import numpy as np, ml_dtypes
CORES = [2,6,10,14,18,22,26,30]
N = 8
import mx_ref
BF = ml_dtypes.bfloat16
def cols(t, e):
    v = np.concatenate([t.reshape(128, -1, 4), np.zeros((128, 1, 4), BF)], axis=1)
    return np.ascontiguousarray(v[:, e]).reshape(128, -1)
def cut(t, i, w=512):
    return t[:, w * i:w * i + w]
def pick(q, e):
    c = np.concatenate([q[0].reshape(128, -1, 4), np.zeros((128, 1, 4), np.uint8)], axis=1); s = np.concatenate([q[1], np.ones((16, 1), np.uint8)], axis=1)
    return (np.ascontiguousarray(c[:, e].reshape(128, -1)), np.ascontiguousarray(s[:, e]))
def join(*qs):
    return (np.concatenate([q[0] for q in qs], axis=1), np.concatenate([q[1] for q in qs], axis=1))
def put(q, e, v):
    c, s = q[0].reshape(128, -1, 4).copy(), q[1].copy(); c[:, e] = v[0].reshape(128, -1, 4); s[:, e] = v[1]
    return (c.reshape(128, -1), s)
def pk(c, s):
    return (np.ascontiguousarray(c), mx_ref.live(s))
def emit(q):
    return q[0], q[1]
def decode(q):
    o = []
    for b in range(4):
        e = np.zeros((128, 128, 4), np.float32); e[np.arange(128), np.arange(128), b] = 1
        o.append(mx_ref.matmul(mx_ref.quantize(e.reshape(128, 512).astype(BF)), q))
    return np.stack(o, axis=2).reshape(128, -1)
def f(rng, *shape):
    return mx_ref.flush((rng.standard_normal(shape, dtype=np.float32) * np.exp2(rng.integers(-2, 3, shape[:-1] + (1,)))).astype(BF))
def wide(rng, *shape, cols=0):
    v = rng.standard_normal(shape, dtype=np.float32) * np.exp2(rng.integers(-12, 13, shape)).astype(np.float32)
    if cols: v *= np.repeat(np.exp2(rng.integers(-cols, cols + 1, shape[:-2] + (1, shape[-1] // 4))) * (rng.random(shape[:-2] + (1, shape[-1] // 4)) > 0.0625), 4, axis=-1).astype(np.float32)
    return mx_ref.flush(v.astype(BF))
M, A, E, R, O = 256, 16, 32, 2, 1
def big(v):
    v = v.astype(np.float32)
    v[np.abs(v) < np.float32(2.0 ** -14)] = 0
    return v.astype(BF)
def plain(rng):
    return {"me": big(f(rng, N, 128, 4 * M)), "x": big(f(rng, N, 128, 4 * A)), "w": f(rng, N, 128, 512 * O)}
def signs(rng, n):
    h = np.ones((1, 1))
    while len(h) < n: h = np.block([[h, h], [h, -h]])
    return h[rng.permutation(n)[:128]][:, rng.permutation(n)] * rng.choice([-1.0, 1.0], n)
def tiles(v):
    return v.reshape(-1, 128, 4).transpose(1, 0, 2).reshape(128, -1)
def store(rng, m, q):
    return {"me": big(np.stack([tiles(v) for v in m.reshape(N, M, 512)])), "x": big(np.stack([tiles(v) for v in q.reshape(N, A, 512)])), "w": f(rng, N, 128, 512 * O)}
def low(rng):
    return rng.standard_normal((N * M, 512), dtype=np.float32) * np.float32(2.0 ** -6)
def rough(rng, v):
    return v * (1 + 0.0625 * rng.uniform(-1, 1, v.shape)) * np.exp2(rng.integers(0, 2, (len(v), 1)))
def places(rng, s):
    at = np.zeros(len(s), int)
    for r in range(N):
        j = np.flatnonzero(s == r)
        at[j] = r * M + rng.permutation(M)[:len(j)]
    return at
def spare(rng, r, at):
    return rng.permutation(np.setdiff1d(np.arange(r * M, r * M + M), at))
def planted(rng, at, o):
    k, i = np.unique(at, return_inverse=True)
    v, m = signs(rng, 512), low(rng)
    m[k] = rough(rng, v[:len(k)])
    m[at[o[0]]] *= 8
    q = rough(rng, v[i])
    q[o[0]] = 4 * v[i[o[0]]] + 8 * v[i[o[-1]]]
    q[o[2]] = q[o[1]]
    return store(rng, m, q)
def setup_inputs(rng):
    return plain(rng)
def setup_inputs_hot(rng):
    h = int(rng.integers(0, N))
    g = (h + int(rng.integers(1, N))) % N
    at = (h + rng.integers(1, N, 128)) % N * M + rng.integers(0, M, 128)
    o = np.flatnonzero(np.arange(128) // A != h)
    p, u = h * M + rng.permutation(M)[:7], g * M + rng.permutation(M)[:6]
    at[o] = u[rng.integers(0, 6, len(o))]
    k = np.concatenate([o[:A], rng.permutation(o[A:-1])[:len(o) // 2 - A - 1]])
    at[k] = p[rng.integers(0, 6, len(k))]
    at[o[2]] = at[o[1]]
    at[o[-1]] = p[6]
    return planted(rng, at, o)
def setup_inputs_ties(rng):
    d, b = plain(rng), int(rng.integers(2, N))
    g = np.full((N, 4), 4.0)
    g[b] = 1
    g[(b + int(rng.integers(1, N))) % N] = 16
    p = big(np.abs(f(rng, 128, 16 * N).astype(np.float32)) * np.repeat(g.reshape(-1), 4))
    k = f(rng, 128, 120).astype(np.float32)
    k[:, :96] = np.abs(k[:, :96])
    k[:, :48] = -k[:, :48]
    k[:, :16] = k[:, :16] * np.float32(2.0 ** 24)
    k = big(k)
    e = rng.permutation(np.concatenate([np.arange(30), rng.integers(12, 24, 58), rng.integers(0, 30, 40)]))
    m = []
    for r in range(N):
        own = np.concatenate([4 * r + np.arange(4), 4 * ((r + 1) % N) + np.arange(4)])
        m.append(cols(p, rng.permutation(np.concatenate([own, own, own[rng.integers(0, 8, M - 16)]]))))
    d["me"] = np.stack(m)
    d["x"] = np.stack([cols(k, e[r * A:r * A + A]) for r in range(N)])
    return d
def setup_inputs_second(rng):
    a, b = signs(rng, 256), signs(rng, 256)
    s = rng.permutation(np.arange(128) % N)
    p = places(rng, np.concatenate([s, (s + rng.integers(1, N, 128)) % N]))
    e = rng.permutation(512)
    e, g = e[:256], e[256:]
    m, q = low(rng), rng.uniform(-1, 1, (128, 512)) * 2.0 ** -6
    q[:, e] = a
    m[p[:128, None], e] = a
    m[p[:128, None], g] = 4 * b
    m[p[128:, None], g] = 16 * b
    return store(rng, m, q)
def setup_inputs_idle(rng):
    o = rng.permutation(N)
    s = o[rng.integers(2, N, 128)]
    s[rng.permutation(128)[:E]] = o[1]
    at = places(rng, s)
    j = int(np.argmin(s))
    z = np.sort(spare(rng, int(s[j]), at)[:2])
    at[j] = z[0]
    far = spare(rng, int(s.max()), at)[0]
    v, m = signs(rng, 512), low(rng)
    v = v * v[j]
    m[at] = rough(rng, v)
    m = m - np.float32(0.25)
    m[[z[0], z[1], far]] = 0
    q = rough(rng, v)
    q[j] = 2 * q[j]
    d = store(rng, m * np.float32(2.0 ** 27), q * 2.0 ** 27)
    c = 4 * int(z[0] % M)
    d["me"][int(s[j]), :, c:c + 4] = BF(-0.0)
    return d
def setup_inputs_spread(rng):
    return {**plain(rng), "me": big(wide(rng, N, 128, 4 * M, cols=3)), "x": big(wide(rng, N, 128, 4 * A, cols=3))}
def check_inputs(d):
    b = []
    for k, least in (("me", 2.0 ** -14), ("x", 2.0 ** -14), ("w", 2.0 ** -30)):
        v = np.abs(d[k].astype(np.float32))
        if not (np.isfinite(v).all() and ((v == 0) | (v >= least) & (v <= 2.0 ** 30)).all()): b.append("a value of " + k)
    return b
def reference(me, x, w):
    mem = [mx_ref.quantize(np.ascontiguousarray(me[r])) for r in range(N)]
    q = join(*[mx_ref.quantize(np.ascontiguousarray(x[r])) for r in range(N)])
    wi = np.zeros((N, R, 128), np.float32)
    for t in range(R):
        s = np.concatenate([mx_ref.matmul(q, mem[r]) for r in range(N)], axis=1) + np.float32(0)
        win = np.argmax(s, axis=1)
        answered = np.zeros(128, bool)
        for r in range(N): answered[np.flatnonzero(win // M == r)[:E]] = True
        wi[:, t] = np.where(answered, win, -1 - win)
        half = decode(pick(join(*mem), win)) * np.float32(0.5)
        new = mx_ref.quantize((half + decode(q) * np.float32(0.5)).astype(BF))
        a = np.flatnonzero(answered)
        q = put(q, a, pick(new, a))
        for r in range(N):
            j = a[win[a] // M == r]
            if j.size:
                c, i = np.unique(win[j] - r * M, return_index=True)
                mem[r] = put(mem[r], c, pick(new, j[i]))
    oc, osc, y = np.zeros((N, 128, 4 * M), np.uint8), np.zeros((N, 16, M), np.uint8), np.zeros((N, 128, 128 * O), np.float32)
    for r in range(N):
        oc[r], osc[r] = emit(mem[r])
        for o in range(O): y[r, :, 128 * o:128 * o + 128] = mx_ref.matmul(mx_ref.quantize(np.ascontiguousarray(cut(w[r], o))), q)
    return {"oc": oc, "osc": osc, "wi": wi, "y": y}

@@ -1,0 +1,381 @@
+from concourse.bass import DstId, RemoteDMATransfer
+from concourse.mybir import dt, AluOpType, AxisListType, ActivationFunctionType
+
+N, M, A, E, R = 8, 256, 16, 32, 2
+NQ = N * A
+OP = AluOpType
+AF = ActivationFunctionType
+AX = AxisListType.X
+BIG = 1.0e9
+LOW = -9.0e29
+
+WORK = [("ti", 32), ("tw", 32), ("to", 32), ("tit", 32), ("twt", 32), ("tot", 32), ("sg", 256), ("wx", 128), ("wy", 128),
+        ("rl", 8), ("sl", 8), ("rw", 128), ("fl", 128), ("cn", 128), ("sa", 128), ("sb", 128), ("acc", 8), ("eqm", 128),
+        ("eqt", 128), ("kk", 8), ("an", 8), ("t1", 8), ("tt", 8), ("ro", 128), ("ox", 128), ("oy", 128), ("m1", 16),
+        ("m2", 16), ("m3", 16), ("m4", 16), ("oh", 8), ("ol", 8), ("ix", 8), ("gg", 8), ("b1", 8), ("b2", 8),
+        ("ab", 512), ("am", 512)]
+AT = {}
+_n = 0
+for _name, _w in WORK:
+    AT[_name] = (_n, _w)
+    _n += _w
+
+SCRATCH = {
+    "xt": ("sbuf", [128, 512], "bfloat16"), "met": ("sbuf", [128, 4 * M], "bfloat16"),
+    "wt": ("sbuf", [128, 512], "bfloat16"), "et": ("sbuf", [128, 2048], "bfloat16"),
+    "half": ("sbuf", [128, 128], "bfloat16"), "diag": ("sbuf", [128, 128], "bfloat16"),
+    "xq": ("sbuf", [128, 128], "float8_e4m3fn_x4"), "xs": ("sbuf", [128, 128], "uint8"),
+    "wq": ("sbuf", [128, 128], "float8_e4m3fn_x4"), "wz": ("sbuf", [128, 128], "uint8"),
+    "eq": ("sbuf", [128, 512], "float8_e4m3fn_x4"), "ez": ("sbuf", [128, 512], "uint8"),
+    "one": ("sbuf", [128, 128], "float32"), "tri": ("sbuf", [128, 128], "float32"),
+    "zz": ("sbuf", [128, 256], "float32"), "wm": ("sbuf", [128, 128], "float32"), "nwm": ("sbuf", [128, 128], "float32"),
+    "rst": ("sbuf", [128, 512], "float32"), "lp": ("sbuf", [128, 128], "int32"), "la": ("sbuf", [128, 128], "int32"),
+    "ip": ("sbuf", [128, 8], "int32"), "ia": ("sbuf", [128, 8], "int32"), "kf": ("sbuf", [128, 32], "float32"),
+    "kq": ("sbuf", [128, 32], "float32"), "c16": ("sbuf", [128, 16], "float32"), "cp": ("sbuf", [128, 16], "float32"),
+    "cn": ("sbuf", [128, 16], "float32"), "cst": ("sbuf", [128, 32], "float32"), "yt": ("sbuf", [128, 128], "float32"),
+    "psc": ("psum", [128, 512], "float32"), "pbl": ("psum", [128, 2048], "float32"), "pyy": ("psum", [128, 512], "float32"),
+}
+for _t in range(R + 1):
+    SCRATCH["mq%d" % _t] = ("sbuf", [128, M], "float8_e4m3fn_x4")
+    SCRATCH["mz%d" % _t] = ("sbuf", [128, M], "uint8")
+    SCRATCH["qa%d" % _t] = ("sbuf", [128, NQ], "float8_e4m3fn_x4")
+    SCRATCH["qz%d" % _t] = ("sbuf", [128, NQ], "uint8")
+for _t in range(R):
+    for _name, _w, _d in (("mw", M + E, "float8_e4m3fn_x4"), ("mx", M + E, "uint8"),
+                          ("win", NQ + N * E, "float8_e4m3fn_x4"), ("wis", NQ + N * E, "uint8"),
+                          ("pm", NQ, "float8_e4m3fn_x4"), ("pz", NQ, "uint8"),
+                          ("nq", 160, "float8_e4m3fn_x4"), ("nz", 160, "uint8"),
+                          ("nt", 520, "bfloat16"), ("run", 264, "float32"), ("land", 32, "float32"),
+                          ("ri", 136, "float32"), ("uu", 32, "float32"), ("wv", 8, "float32"), ("f", _n, "float32"),
+                          ("offi", 8, "uint16"), ("offs", 2, "uint16"), ("offm", 16, "uint16"), ("offq", 8, "uint16")):
+        SCRATCH["%s%d" % (_name, _t)] = ("sbuf", [128, _w], _d)
+SCRATCH["lidx"] = ("sbuf", [128, 32], "float32")
+
+ONCE = ["ldx", "ldm", "ldw", "ixt", "ihf", "ion", "gdi", "gip", "gtr", "g16", "xqd", "eqd", "wqd", "qx", "oq", "mq0", "vcc",
+        "ls", "idx", "oli", "yp", "yc", "st"]
+EACH = ["sc", "rn", "ix", "ow", "it", "ib", "oi", "pm", "ba", "bb", "bc", "bd", "nt", "nq", "ar", "rl", "wr", "wt", "wb", "ct",
+        "ac", "os", "sl", "u1", "ab", "ot", "ob", "om", "mp", "od", "nx", "on", "qp", "vc", "mc", "qc", "wi"]
+SEMAPHORES = ONCE + ["%s%d" % (_s, _t) for _s in EACH for _t in range(R)]
+
+
+def rank_program(g, core, T, topo):
+    rank = T.rank_of(core)
+    if rank is None:
+        return
+    V, S, P, Y = g.vector, g.scalar, g.tensor, g.sync
+    queue = {"v": V, "s": S, "t": P, "y": Y, "g": g}
+    total, seen = {}, {}
+
+    def up(ins, name, n=1):
+        ins.then_inc(T.sem[name], n)
+        total[name] = total.get(name, 0) + n
+
+    def wait(q, *names):
+        for name in names:
+            if seen.get((q, name), 0) < total[name]:
+                queue[q].wait_ge(T.sem[name], total[name])
+                seen[(q, name)] = total[name]
+                seen[("", name)] = total[name]
+
+    def u32(name, a, b):
+        return T[name][:, a:b].bitcast(dt.uint32)
+
+    def u8(name, a, b):
+        return T[name][:, a:b].bitcast(dt.uint8)
+
+    here = topo.chip(core)
+
+    def near(c):
+        k = topo.chip(c)
+        return (2 if topo.mates(here, k) else 1 if topo.same_plane(here, k) else 0, topo.die(c) != topo.die(core))
+
+    off = sorted([c for c in T.cores if topo.chip(c) != here], key=near)
+    on = [c for c in T.cores if c != core and topo.chip(c) == here]
+    common = topo.mask(core, off[0])
+    for c in off:
+        common = common & topo.mask(core, c)
+    free = [e for e in topo.engines(core, on[0]) if not common >> e & 1]
+    local = (1 << free[0]) | (1 << free[len(free) // 2])
+    n_off = sum(common >> e & 1 for e in range(common.bit_length()))
+    arrive = len(off) * n_off + len(on) * 2
+
+    def dst(c):
+        rid, pid = topo.addr(c)[:2]
+        return DstId(rid=rid, pnc=pid)
+
+    def send(src, out, sem):
+        g.remote_dma_fused([
+            RemoteDMATransfer(dst_ids=[dst(c) for c in off], dma_engine_mask=common, remote_sem=T.sem[sem],
+                              srcs=[src], dsts=[out for c in off]),
+            RemoteDMATransfer(dst_ids=[dst(c) for c in on], dma_engine_mask=local, remote_sem=T.sem[sem],
+                              srcs=[src], dsts=[out for c in on])], local_sem=T.sem["ls"])
+        total["ls"] = total.get("ls", 0) + n_off + 2
+        total[sem] = total.get(sem, 0) + arrive
+
+    up(Y.dma_start(T.xt[:, 0:4 * A], T.x[:]), "ldx", 16)
+    up(S.dma_start(T.met[:], T.me[:]), "ldm", 16)
+    up(S.dma_start(T.wt[:], T.w[:]), "ldw", 16)
+
+    up(V.memset(T.xt[:, 4 * A:512], 0.0), "ixt")
+    up(V.memset(T.half[:], 0.5), "ihf")
+    up(V.memset(T.one[:], 1.0), "ion")
+    up(V.memset(T.et[:], 0.0), "vcc")
+    up(g.iota(T.ip[:, 0:1], [[1, 1]], 0, 1), "gip")
+    up(g.iota(T.lp[:], [[1, 128]], 128, -1), "gip")
+    up(g.iota(T.kf[:], [[1, 32]], 0, 0, allow_small_or_imprecise_dtypes=True), "gip")
+    wait("g", "ihf")
+    up(g.affine_select(T.diag[:], T.half[:], [[-1, 128]], OP.is_equal, 0.0, 0, 1), "gdi")
+    wait("v", "ldx", "ixt")
+    up(V.quantize_mx(T.xq[:], T.xs[:], T.xt[:]), "xqd")
+    a = A * rank
+    wait("g", "xqd")
+    send(u8("xq", 0, A), u8("qa0", a, a + A), "qx")
+    send(T.xs[:, 0:A], T.qz0[:, a:a + A], "qx")
+    wait("y", "xqd")
+    up(Y.dma_start(u8("qa0", a, a + A), u8("xq", 0, A)), "oq", 16)
+    up(Y.dma_start(T.qz0[:, a:a + A], T.xs[:, 0:A]), "oq", 16)
+    wait("g", "ion")
+    up(g.iota(T.c16[:], [[16, 16]], 0, 0, allow_small_or_imprecise_dtypes=True), "g16")
+    up(g.affine_select(T.tri[:], T.one[:], [[-1, 128]], OP.is_gt, 0.0, 0, 1), "gtr")
+    wait("g", "gip", "gdi", "g16", "gtr")
+
+    wait("v", "vcc", "gdi")
+    for b in range(4):
+        up(V.tensor_copy(T.et[:, 512 * b + b:512 * b + 512:4], T.diag[:]), "vcc")
+    wait("v", "vcc")
+    up(V.quantize_mx(T.eq[:], T.ez[:], T.et[:]), "eqd")
+    up(V.memset(T.zz[:], 0.0), "vcc")
+    wait("v", "ldm")
+    up(V.quantize_mx(T.mq0[:], T.mz0[:], T.met[:]), "mq0")
+    wait("y", "mq0")
+    up(Y.dma_start(u8("mw0", 0, M), u8("mq0", 0, M)), "mc0", 16)
+    up(Y.dma_start(T.mx0[:, 0:M], T.mz0[:]), "mc0", 16)
+    wait("v", "gip")
+    up(V.tensor_scalar(T.la[:], T.lp[:], 15, None, OP.bitwise_and), "vcc")
+    up(V.tensor_scalar(T.ia[:, 0:1], T.ip[:, 0:1], 15, None, OP.bitwise_and), "vcc")
+    up(V.tensor_copy(T.cst[:, 0:1], T.ip[:, 0:1]), "vcc")
+    up(V.tensor_scalar(T.kq[:], T.kf[:], 1.0 / 64, None, OP.mult), "vcc")
+    for t in range(R):
+        f = T["f%d" % t]
+        up(V.memset(f[:, 0:96], 0.0), "vcc")
+        up(V.memset(T["ri%d" % t][:, 128:136], 1000.0), "vcc")
+        up(V.memset(T["nt%d" % t][:, 512:520], 0.0), "vcc")
+    up(V.memset(T.rst[:], -BIG), "vcc")
+    wait("v", "vcc")
+    up(V.memset(T.rst[:, 0:512:32], BIG), "vcc")
+    up(V.tensor_scalar(T.wm[:], T.la[:], 0, None, OP.is_equal), "vcc")
+    up(V.tensor_scalar(T.nwm[:], T.la[:], 0, None, OP.not_equal), "vcc")
+    up(V.tensor_copy(T.cst[:, 1:2], T.ia[:, 0:1]), "vcc")
+    up(V.tensor_scalar(T.cst[:, 2:3], T.cst[:, 0:1], -1.0, float(NQ), OP.mult, OP.add), "vcc")
+    wait("v", "vcc", "g16")
+    up(V.tensor_scalar(T.cst[:, 4:5], T.cst[:, 1:2], 0.5, None, OP.add), "vcc")
+    up(V.tensor_scalar(T.cst[:, 5:6], T.cst[:, 1:2], 16.5, None, OP.add), "vcc")
+    up(V.tensor_scalar(T.cp[:], T.c16[:], T.cst[:, 1:2], None, OP.add), "vcc")
+    up(V.tensor_scalar(T.cn[:], T.c16[:], T.cst[:, 1:2], -1.0, OP.add, OP.mult), "vcc")
+    wait("v", "ldw")
+    up(V.quantize_mx(T.wq[:], T.wz[:], T.wt[:]), "wqd")
+    wait("v", "vcc")
+    wait("y", "qx", "oq")
+    up(Y.dma_start(u8("win0", 0, NQ), u8("qa0", 0, NQ)), "qc0", 16)
+    up(Y.dma_start(T.wis0[:, 0:NQ], T.qz0[:]), "qc0", 16)
+
+    def rows(out, view, sem_in, sem_out):
+        wait("g", sem_in)
+        for k in range(4):
+            up(g.partition_broadcast(out[:, 32 * k:32 * k + 32], view(32 * k, 32 * k + 1), 128), sem_out)
+
+    def wrap(row, f, x, y, out, vc, sem):
+        up(V.tensor_tensor(f(x), row, T.wm[:], OP.mult), vc)
+        wait("v", vc)
+        up(V.tensor_tensor_scan(f(y), T.nwm[:], f(x), 0.0, OP.mult, OP.add), vc)
+        wait("v", vc)
+        up(V.tensor_copy(out[:], f(y, 15, 128, 16)), sem)
+
+    for t in range(R):
+        def B(name, u=t):
+            return T["%s%d" % (name, u)]
+
+        def s(name, u=t):
+            return "%s%d" % (name, u)
+
+        def f(name, a=0, b=None, step=1, u=t):
+            o, w = AT[name]
+            return T["f%d" % u][:, o + a:o + (w if b is None else b):step]
+
+        def fr(name, u=t):
+            o, w = AT[name]
+            return lambda p, q: T["f%d" % u][p:q, o:o + w]
+
+        one = (0, 1)
+        vc = s("vc")
+        mq, mz, qa, qz = B("mq"), B("mz"), B("qa"), B("qz")
+        if t == 0:
+            wait("t", "mq0", "oq", "qx")
+        else:
+            wait("t", s("mp", 0), s("rn", 0), s("qp", 0))
+        up(P.matmul_mx(T.psc[:, 0:M], qa[:], qz[:], mq[:], mz[:], True, True), s("sc"))
+        wait("t", "eqd")
+        if t:
+            wait("t", s("nt", 0))
+        for b in (0, 2, 1, 3):
+            P.matmul_mx(T.pbl[:, 512 * b:512 * b + NQ], T.eq[:, 128 * b:128 * b + 128], T.ez[:, 128 * b:128 * b + 128],
+                        qa[:], qz[:], True, False)
+        run = B("run")
+        wait("v", s("sc"))
+        up(V.tensor_tensor_scan(run[:, 0:M], T.psc[:, 0:M], T.zz[:], LOW, OP.max, OP.add), s("rn"))
+        land = B("land")
+        k = 4 * rank
+        if t == 0:
+            wait("g", s("rn"))
+            send(run[:, M - 1:M], land[:, k:k + 1], s("ar"))
+        else:
+            wait("g", s("ow", 0), s("rn"))
+            send(run[:, M - 1:M + 1], land[:, k:k + 2], s("ar"))
+        wait("s", s("rn"))
+        up(S.activation(f("sg"), run[:, 0:M], AF.Sign, bias=run[:, M - 1:M], scale=-1.0, accum_out=f("ti", *one)), s("ix"))
+        up(S.activation(land[:, k:k + 1], run[:, M - 1:M], AF.Copy), s("ow"))
+        wait("s", s("ix"))
+        if t == 0:
+            up(S.activation(T.run1[:, M:M + 1], f("ti", *one), AF.Copy), s("ow"))
+            up(S.activation(T.land1[:, k + 1:k + 2], f("ti", *one), AF.Copy), s("ow"))
+        else:
+            up(S.activation(T.lidx[:, k:k + 1], f("ti", *one), AF.Copy), "oli")
+        wait("v", s("ix"))
+        up(V.transpose(f("tit"), f("ti")), s("it"))
+        ri = B("ri")
+        rows(ri, fr("tit"), s("it"), s("ib"))
+        if t:
+            wait("g", s("ix"))
+            send(f("ti", *one), T.lidx[:, k:k + 1], "idx")
+        wait("v", s("ib"))
+        wrap(ri[:, 0:128], f, "wx", "wy", B("offi"), vc, s("oi"))
+        wait("v", s("oi"))
+        up(V.tensor_copy(u32(s("pm"), 0, NQ), u32(s("mq"), 0, M).indirect(B("offi")[:, 0:8])), s("pm"))
+        wait("s", s("oi"))
+        up(S.activation(B("pz")[:, 0:NQ], mz[:, 0:M].indirect(B("offi")[:, 0:8]), AF.Copy), s("pm"))
+        wait("t", s("pm"))
+        bank = {0: s("ba"), 1: s("bb"), 2: s("bc"), 3: s("bd")}
+        for b in (0, 2, 1, 3):
+            up(P.matmul_mx(T.pbl[:, 512 * b:512 * b + NQ], T.eq[:, 128 * b:128 * b + 128], T.ez[:, 128 * b:128 * b + 128],
+                           B("pm")[:], B("pz")[:], False, True), bank[b])
+        wait("v", s("ow"), s("ar"))
+        up(V.tensor_tensor_scan(f("rl"), land[:, 0:32:4], T.zz[:, 0:8], LOW, OP.max, OP.add), s("rl"))
+        wait("s", s("rl"))
+        up(S.activation(f("sl"), f("rl"), AF.Sign, bias=f("rl", 7, 8), scale=-1.0, accum_out=f("tw", *one)), s("wr"))
+        wait("v", s("wr"))
+        up(V.transpose(f("twt"), f("tw")), s("wt"))
+        rows(f("rw"), fr("twt"), s("wt"), s("wb"))
+        nt = B("nt")
+        for b in (0, 1):
+            wait("v", bank[b])
+            up(V.tensor_copy(nt[:, b:512:4], T.pbl[:, 512 * b:512 * b + NQ]), s("nt"))
+        for b in (2, 3):
+            wait("s", bank[b])
+            up(S.activation(nt[:, b:512:4], T.pbl[:, 512 * b:512 * b + NQ], AF.Copy), s("nt"))
+        wait("v", s("nt"))
+        up(V.quantize_mx(B("nq")[:, 0:130], B("nz")[:, 0:130], nt[:]), s("nq"))
+        wait("v", s("wb"))
+        up(V.tensor_scalar(f("fl"), f("rw"), float(rank), None, OP.is_equal), vc)
+        wait("v", vc)
+        up(V.tensor_tensor_scan(f("cn"), f("fl"), T.zz[:, 0:128], 0.0, OP.add, OP.add), s("ct"))
+        wait("s", s("ct"))
+        up(S.activation(f("sa"), f("cn"), AF.Sign, bias=T.cst[:, 4:5], scale=-1.0, accum_out=f("acc", 0, 1)), s("ac"))
+        up(S.activation(f("sb"), f("cn"), AF.Sign, bias=T.cst[:, 5:6], scale=-1.0, accum_out=f("acc", 1, 2)), s("ac"))
+        wait("v", s("nq"), s("mc"), s("ac"))
+        offs = B("offs")
+        up(V.tensor_scalar(offs[:, 0:2], f("acc", 0, 2), 0.5, 64.0, OP.mult, OP.add), s("os"))
+        wait("v", s("os"))
+        up(V.tensor_copy(u32(s("mw"), M, M + E), u32(s("nq"), 0, 130).indirect(offs[:, 0:2])), s("sl"))
+        wait("s", s("nq"), s("mc"), s("os"))
+        up(S.activation(B("mx")[:, M:M + E], B("nz")[:, 0:130].indirect(offs[:, 0:2]), AF.Copy), s("sl"))
+        wait("g", s("sl"))
+        e = NQ + E * rank
+        send(u8(s("mw"), M, M + E), u8(s("win"), e, e + E), s("nx"))
+        send(B("mx")[:, M:M + E], B("wis")[:, e:e + E], s("nx"))
+        wait("y", s("sl"))
+        up(Y.dma_start(u8(s("win"), e, e + E), u8(s("mw"), M, M + E)), s("on"), 16)
+        up(Y.dma_start(B("wis")[:, e:e + E], B("mx")[:, M:M + E]), s("on"), 16)
+        w = f("tw", *one)
+        wait("v", "gtr")
+        up(V.tensor_scalar(f("eqm"), f("rw"), w, None, OP.is_equal), vc)
+        up(V.tensor_scalar(f("t1", *one), w, float(E), T.cst[:, 2:3], OP.mult, OP.add), vc)
+        up(V.tensor_tensor(B("uu")[:, 0:E], ri[:, 0:136].indirect(offs[:, 0:2]), T.kq[:], OP.add), s("u1"))
+        wait("v", vc)
+        up(V.tensor_tensor(f("eqt"), f("eqm"), T.tri[:], OP.mult), vc)
+        wait("v", vc)
+        up(V.tensor_reduce(f("kk", *one), f("eqt"), AX, OP.add), vc)
+        wait("v", vc)
+        up(V.tensor_scalar(f("an", *one), f("kk", *one), float(E), None, OP.is_lt), vc)
+        wait("v", vc)
+        up(V.tensor_scalar(f("tt", *one), f("kk", *one), f("t1", *one), f("an", *one), OP.add, OP.mult), vc)
+        wait("v", vc)
+        up(V.tensor_scalar(f("to", *one), f("tt", *one), T.cst[:, 0:1], None, OP.add), vc)
+        wait("v", vc)
+        up(V.transpose(f("tot"), f("to")), s("ot"))
+        rows(f("ro"), fr("tot"), s("ot"), s("ob"))
+        wait("s", s("u1"))
+        for c in range(16):
+            up(S.activation(f("ab", 32 * c, 32 * c + 32), B("uu")[:, 0:E], AF.Abs, bias=T.cn[:, c:c + 1], scale=1.0), s("ab"))
+        wait("v", s("ab"))
+        up(V.tensor_tensor_scan(f("am"), T.rst[:], f("ab"), 0.0, OP.max, OP.min), vc)
+        wait("v", vc)
+        low = f("am", 31, 512, 32)
+        up(V.tensor_scalar(f("m1"), low, 0.5, None, OP.is_lt), vc)
+        up(V.tensor_scalar(f("m2"), low, 64.0, float(M), OP.mult, OP.add), vc)
+        wait("v", vc)
+        up(V.tensor_tensor(f("m3"), f("m1"), f("m2"), OP.mult), vc)
+        wait("v", vc)
+        up(V.tensor_tensor(f("m4"), f("m3"), T.cp[:], OP.max), vc)
+        wait("v", vc)
+        up(V.tensor_copy(B("offm")[:], f("m4")), s("om"))
+        wait("v", s("ob"))
+        wrap(f("ro"), f, "ox", "oy", B("offq"), vc, s("od"))
+        wait("v", s("om"), s("sl"))
+        mp = s("mp")
+        up(V.tensor_copy(u32(s("mq", t + 1), 0, M), u32(s("mw"), 0, M + E).indirect(B("offm")[:, 0:16])), mp)
+        wait("s", s("om"), s("sl"))
+        up(S.activation(B("mz", t + 1)[:, 0:M], B("mx")[:, 0:M + E].indirect(B("offm")[:, 0:16]), AF.Copy), mp)
+        wait("y", mp)
+        if t + 1 < R:
+            up(Y.dma_start(u8("mw1", 0, M), u8("mq1", 0, M)), "mc1", 16)
+            up(Y.dma_start(T.mx1[:, 0:M], T.mz1[:]), "mc1", 16)
+        else:
+            up(Y.dma_start(T.oc[:, 0:4 * M], u8(s("mq", R), 0, M)), "st", 16)
+            for c in range(4):
+                up(Y.dma_start(T.osc[4 * c:4 * c + 4, 0:M], B("mz", R)[32 * c:32 * c + 4, 0:M]), "st", 16)
+            wait("v", "idx", "oli")
+            for u in range(R):
+                where = T.land1[:, 1:32:4] if u == 0 else T.lidx[:, 0:32:4]
+                wu, au = f("tw", 0, 1, 1, u), f("an", 0, 1, 1, u)
+                up(V.tensor_scalar(f("oh", 0, 8, 1, u), T.kf[:, 0:8], wu, None, OP.is_equal), vc)
+                up(V.tensor_scalar(f("b2", 0, 1, 1, u), au, 2.0, -1.0, OP.mult, OP.add), vc)
+                up(V.tensor_scalar(f("b1", 0, 1, 1, u), au, -1.0, None, OP.add), vc)
+                wait("v", vc)
+                up(V.tensor_tensor(f("ol", 0, 8, 1, u), f("oh", 0, 8, 1, u), where, OP.mult), vc)
+                wait("v", vc)
+                up(V.tensor_reduce(f("ix", 0, 1, 1, u), f("ol", 0, 8, 1, u), AX, OP.add), vc)
+                wait("v", vc)
+                up(V.tensor_scalar(f("gg", 0, 1, 1, u), wu, float(M), f("ix", 0, 1, 1, u), OP.mult, OP.add), vc)
+                wait("v", vc)
+                up(V.tensor_scalar(B("wv", u)[:, 0:1], f("gg", 0, 1, 1, u), f("b2", 0, 1, 1, u), f("b1", 0, 1, 1, u),
+                                   OP.mult, OP.add), s("wi", u))
+                wait("y", s("wi", u))
+                up(Y.dma_start(T.wi[u:u + 1, :], B("wv", u)[:, 0:1]), "st", 16)
+        for q in ("v", "s"):
+            wait(q, s("od"), s("on"), s("qc"), s("nx"))
+        up(V.tensor_copy(u32(s("qa", t + 1), 0, NQ), u32(s("win"), 0, NQ + N * E).indirect(B("offq")[:, 0:8])), s("qp"))
+        up(S.activation(B("qz", t + 1)[:, 0:NQ], B("wis")[:, 0:NQ + N * E].indirect(B("offq")[:, 0:8]), AF.Copy), s("qp"))
+        if t + 1 < R:
+            wait("y", s("qp"))
+            up(Y.dma_start(u8("win1", 0, NQ), u8("qa1", 0, NQ)), "qc1", 16)
+            up(Y.dma_start(T.wis1[:, 0:NQ], T.qz1[:]), "qc1", 16)
+
+    wait("t", "wqd", "qp1")
+    up(P.matmul_mx(T.pyy[:, 0:NQ], T.wq[:], T.wz[:], T.qa2[:], T.qz2[:], True, True), "yp")
+    wait("v", "yp")
+    up(V.tensor_copy(T.yt[:], T.pyy[:, 0:NQ]), "yc")
+    wait("y", "yc")
+    up(Y.dma_start(T.y[:], T.yt[:]), "st", 16)
+    for name in total:
+        if seen.get(("", name), 0) < total[name]:
+            wait("g", name)

@@ -8,12 +8,12 @@ AF = ActivationFunctionType
 AX = AxisListType.X
 BIG = 1.0e9
 LOW = -9.0e29
+OUT = 65536.0
 
-WORK = [("ti", 32), ("tw", 32), ("to", 32), ("tit", 32), ("twt", 32), ("tot", 32), ("sg", 256), ("wx", 128), ("wy", 128),
-        ("rl", 8), ("sl", 8), ("rw", 128), ("fl", 128), ("cn", 128), ("sa", 128), ("sb", 128), ("acc", 8), ("eqm", 128),
-        ("eqt", 128), ("kk", 8), ("an", 8), ("t1", 8), ("tt", 8), ("ro", 128), ("ox", 128), ("oy", 128), ("m1", 16),
-        ("m2", 16), ("m3", 16), ("m4", 16), ("oh", 8), ("ol", 8), ("ix", 8), ("gg", 8), ("b1", 8), ("b2", 8),
-        ("ab", 512), ("am", 512)]
+WORK = [("ti", 8), ("sl", 16), ("ra", 32), ("ru", 32), ("fr", 32), ("oh", 32), ("cb", 32), ("rc", 32), ("la", 128),
+        ("ly", 128), ("ft", 128), ("cn", 128), ("sa", 128), ("sb", 128), ("acc", 8), ("ot", 128), ("ct", 128), ("lc", 128),
+        ("oy", 128), ("rl", 8), ("tw", 8), ("t1", 8), ("kr", 8), ("kk", 8), ("an", 8), ("tt", 8), ("m1", 8), ("m2", 8),
+        ("m3", 8), ("m4", 8), ("ol", 8), ("ix", 8), ("gg", 8), ("b1", 8), ("b2", 8), ("sg", 256), ("ab", 256), ("am", 256)]
 AT = {}
 _n = 0
 for _name, _w in WORK:
@@ -27,12 +27,14 @@ SCRATCH = {
     "xq": ("sbuf", [128, 128], "float8_e4m3fn_x4"), "xs": ("sbuf", [128, 128], "uint8"),
     "wq": ("sbuf", [128, 128], "float8_e4m3fn_x4"), "wz": ("sbuf", [128, 128], "uint8"),
     "eq": ("sbuf", [128, 512], "float8_e4m3fn_x4"), "ez": ("sbuf", [128, 512], "uint8"),
-    "one": ("sbuf", [128, 128], "float32"), "tri": ("sbuf", [128, 128], "float32"),
-    "zz": ("sbuf", [128, 256], "float32"), "wm": ("sbuf", [128, 128], "float32"), "nwm": ("sbuf", [128, 128], "float32"),
-    "rst": ("sbuf", [128, 512], "float32"), "lp": ("sbuf", [128, 128], "int32"), "la": ("sbuf", [128, 128], "int32"),
+    "zz": ("sbuf", [128, 256], "float32"), "wm": ("sbuf", [128, 32], "float32"), "nwm": ("sbuf", [128, 128], "float32"),
+    "wp": ("sbuf", [128, 32], "float32"),
+    "rst": ("sbuf", [128, 256], "float32"), "lp": ("sbuf", [128, 128], "int32"), "la": ("sbuf", [128, 128], "int32"),
     "ip": ("sbuf", [128, 8], "int32"), "ia": ("sbuf", [128, 8], "int32"), "kf": ("sbuf", [128, 32], "float32"),
     "kq": ("sbuf", [128, 32], "float32"), "c16": ("sbuf", [128, 16], "float32"), "cp": ("sbuf", [128, 16], "float32"),
-    "cn": ("sbuf", [128, 16], "float32"), "cst": ("sbuf", [128, 32], "float32"), "yt": ("sbuf", [128, 128], "float32"),
+    "cc": ("sbuf", [128, 8], "float32"), "cn": ("sbuf", [128, 8], "float32"),
+    "cst": ("sbuf", [128, 32], "float32"), "yt": ("sbuf", [128, 128], "float32"),
+    "idl": ("sbuf", [128, 16], "uint16"), "lidx": ("sbuf", [128, 32], "float32"),
     "psc": ("psum", [128, 512], "float32"), "pbl": ("psum", [128, 2048], "float32"), "pyy": ("psum", [128, 512], "float32"),
 }
 for _t in range(R + 1):
@@ -49,13 +51,13 @@ for _t in range(R):
                           ("ri", 136, "float32"), ("uu", 32, "float32"), ("wv", 8, "float32"), ("f", _n, "float32"),
                           ("offi", 8, "uint16"), ("offs", 2, "uint16"), ("offm", 16, "uint16"), ("offq", 8, "uint16")):
         SCRATCH["%s%d" % (_name, _t)] = ("sbuf", [128, _w], _d)
-SCRATCH["lidx"] = ("sbuf", [128, 32], "float32")
 
-ONCE = ["ldx", "ldm", "ldw", "ixt", "ihf", "ion", "gdi", "gip", "gtr", "g16", "xqd", "eqd", "wqd", "qx", "oq", "mq0", "vcc",
-        "ls", "idx", "oli", "yp", "yc", "st"]
-EACH = ["sc", "rn", "ix", "ow", "it", "ib", "oi", "pm", "ba", "bb", "bc", "bd", "nt", "nq", "ar", "rl", "wr", "wt", "wb", "ct",
-        "ac", "os", "sl", "u1", "ab", "ot", "ob", "om", "mp", "od", "nx", "on", "qp", "vc", "mc", "qc", "wi"]
+ONCE = ["ldx", "ldm", "ldw", "ixt", "ihf", "gdi", "gip", "xqd", "eqd", "wqd", "qx", "oq", "mq0", "vcc", "vco", "vid",
+        "ls", "idx", "oli", "orn", "yp", "yc", "st", "sty"]
+EACH = ["sc", "rn", "ix", "ow", "oi", "pm", "ba", "bb", "bc", "bd", "nt", "nq", "ar", "ac", "os", "sl", "u1", "ab",
+        "om", "mp", "od", "nx", "on", "qp", "mc", "qc", "wi", "va", "vu", "vb", "vk", "vc", "vm", "vw"]
 SEMAPHORES = ONCE + ["%s%d" % (_s, _t) for _s in EACH for _t in range(R)]
+QUARTERS = (0, 32, 64, 96)
 
 
 def rank_program(g, core, T, topo):
@@ -113,14 +115,14 @@ def rank_program(g, core, T, topo):
         total[sem] = total.get(sem, 0) + arrive
 
     up(Y.dma_start(T.xt[:, 0:4 * A], T.x[:]), "ldx", 16)
-    up(S.dma_start(T.met[:], T.me[:]), "ldm", 16)
-    up(S.dma_start(T.wt[:], T.w[:]), "ldw", 16)
+    up(Y.dma_start(T.met[:], T.me[:]), "ldm", 16)
+    up(Y.dma_start(T.wt[:], T.w[:]), "ldw", 16)
 
     up(V.memset(T.xt[:, 4 * A:512], 0.0), "ixt")
     up(V.memset(T.half[:], 0.5), "ihf")
-    up(V.memset(T.one[:], 1.0), "ion")
     up(V.memset(T.et[:], 0.0), "vcc")
     up(g.iota(T.ip[:, 0:1], [[1, 1]], 0, 1), "gip")
+    up(g.iota(T.c16[:], [[16, 16]], 0, 0, allow_small_or_imprecise_dtypes=True), "gip")
     up(g.iota(T.lp[:], [[1, 128]], 128, -1), "gip")
     up(g.iota(T.kf[:], [[1, 32]], 0, 0, allow_small_or_imprecise_dtypes=True), "gip")
     wait("g", "ihf")
@@ -131,65 +133,60 @@ def rank_program(g, core, T, topo):
     wait("g", "xqd")
     send(u8("xq", 0, A), u8("qa0", a, a + A), "qx")
     send(T.xs[:, 0:A], T.qz0[:, a:a + A], "qx")
-    wait("y", "xqd")
-    up(Y.dma_start(u8("qa0", a, a + A), u8("xq", 0, A)), "oq", 16)
-    up(Y.dma_start(T.qz0[:, a:a + A], T.xs[:, 0:A]), "oq", 16)
-    wait("g", "ion")
-    up(g.iota(T.c16[:], [[16, 16]], 0, 0, allow_small_or_imprecise_dtypes=True), "g16")
-    up(g.affine_select(T.tri[:], T.one[:], [[-1, 128]], OP.is_gt, 0.0, 0, 1), "gtr")
-    wait("g", "gip", "gdi", "g16", "gtr")
+    wait("g", "gip", "gdi")
 
+    wait("v", "gip")
+    up(V.tensor_scalar(T.ia[:, 0:1], T.ip[:, 0:1], 15, None, OP.bitwise_and), "vid")
+    up(V.tensor_copy(T.cst[:, 0:1], T.ip[:, 0:1]), "vco")
+    up(V.tensor_scalar(T.la[:], T.lp[:], 15, None, OP.bitwise_and), "vco")
+    wait("v", "vid")
+    up(V.tensor_copy(T.cst[:, 1:2], T.ia[:, 0:1]), "vid")
+    wait("v", "vid")
+    up(V.tensor_scalar(T.cp[:], T.c16[:], T.cst[:, 1:2], None, OP.add), "vid")
+    wait("v", "vid")
+    up(V.tensor_copy(T.idl[:], T.cp[:]), "vid")
+    wait("v", "vid", "xqd")
+    up(V.tensor_copy(u32("qa0", a, a + A), u32("xq", 0, NQ).indirect(T.idl[:, 0:1])), "oq")
+    wait("s", "vid", "xqd")
+    up(S.activation(T.qz0[:, a:a + A], T.xs[:, 0:NQ].indirect(T.idl[:, 0:1]), AF.Copy), "oq")
     wait("v", "vcc", "gdi")
     for b in range(4):
         up(V.tensor_copy(T.et[:, 512 * b + b:512 * b + 512:4], T.diag[:]), "vcc")
+    up(V.memset(T.zz[:], 0.0), "vco")
     wait("v", "vcc")
     up(V.quantize_mx(T.eq[:], T.ez[:], T.et[:]), "eqd")
-    up(V.memset(T.zz[:], 0.0), "vcc")
     wait("v", "ldm")
     up(V.quantize_mx(T.mq0[:], T.mz0[:], T.met[:]), "mq0")
-    wait("y", "mq0")
-    up(Y.dma_start(u8("mw0", 0, M), u8("mq0", 0, M)), "mc0", 16)
-    up(Y.dma_start(T.mx0[:, 0:M], T.mz0[:]), "mc0", 16)
-    wait("v", "gip")
-    up(V.tensor_scalar(T.la[:], T.lp[:], 15, None, OP.bitwise_and), "vcc")
-    up(V.tensor_scalar(T.ia[:, 0:1], T.ip[:, 0:1], 15, None, OP.bitwise_and), "vcc")
-    up(V.tensor_copy(T.cst[:, 0:1], T.ip[:, 0:1]), "vcc")
-    up(V.tensor_scalar(T.kq[:], T.kf[:], 1.0 / 64, None, OP.mult), "vcc")
+    up(V.memset(T.rst[:], -BIG), "vco")
     for t in range(R):
-        f = T["f%d" % t]
-        up(V.memset(f[:, 0:96], 0.0), "vcc")
-        up(V.memset(T["ri%d" % t][:, 128:136], 1000.0), "vcc")
-        up(V.memset(T["nt%d" % t][:, 512:520], 0.0), "vcc")
-    up(V.memset(T.rst[:], -BIG), "vcc")
-    wait("v", "vcc")
-    up(V.memset(T.rst[:, 0:512:32], BIG), "vcc")
-    up(V.tensor_scalar(T.wm[:], T.la[:], 0, None, OP.is_equal), "vcc")
-    up(V.tensor_scalar(T.nwm[:], T.la[:], 0, None, OP.not_equal), "vcc")
-    up(V.tensor_copy(T.cst[:, 1:2], T.ia[:, 0:1]), "vcc")
-    up(V.tensor_scalar(T.cst[:, 2:3], T.cst[:, 0:1], -1.0, float(NQ), OP.mult, OP.add), "vcc")
-    wait("v", "vcc", "g16")
-    up(V.tensor_scalar(T.cst[:, 4:5], T.cst[:, 1:2], 0.5, None, OP.add), "vcc")
-    up(V.tensor_scalar(T.cst[:, 5:6], T.cst[:, 1:2], 16.5, None, OP.add), "vcc")
-    up(V.tensor_scalar(T.cp[:], T.c16[:], T.cst[:, 1:2], None, OP.add), "vcc")
-    up(V.tensor_scalar(T.cn[:], T.c16[:], T.cst[:, 1:2], -1.0, OP.add, OP.mult), "vcc")
+        o = AT["oh"][0]
+        up(V.memset(T["f%d" % t][:, o:o + 32], 0.0), "vco")
+        o = AT["sl"][0]
+        up(V.memset(T["f%d" % t][:, o:o + 1], 1.0), "vco")
+        up(V.memset(T["ri%d" % t][:], 1000.0), "vco")
+        up(V.memset(T["nt%d" % t][:, 512:520], 0.0), "vco")
+    up(V.tensor_scalar(T.kq[:], T.kf[:], 1.0 / 64, None, OP.mult), "vco")
+    up(V.tensor_copy(T.cc[0:32, :], T.cp[0:32, 0:8]), "vco")
+    up(V.tensor_copy(T.cc[32:64, :], T.cp[32:64, 8:16]), "vco")
+    wait("v", "mq0")
+    up(V.tensor_copy(u32("mw0", 0, M), u32("mq0", 0, M).indirect(T.idl[:])), "mc0")
+    wait("s", "mq0")
+    up(S.activation(T.mx0[:, 0:M], T.mz0[:].indirect(T.idl[:]), AF.Copy), "mc0")
+    wait("v", "vco")
+    up(V.memset(T.rst[:, 0:256:32], BIG), "vco")
+    up(V.tensor_scalar(T.wm[:], T.la[:, 0:32], 0, None, OP.is_equal), "vco")
+    up(V.tensor_scalar(T.nwm[:], T.la[:], 0, None, OP.not_equal), "vco")
+    up(V.tensor_scalar(T.cst[:, 2:3], T.cst[:, 0:1], -1.0, float(NQ - 1), OP.mult, OP.add), "vco")
+    up(V.tensor_scalar(T.cst[:, 3:4], T.cst[:, 0:1], OUT, None, OP.add), "vco")
+    up(V.tensor_scalar(T.cst[:, 4:5], T.cst[:, 1:2], 0.5, None, OP.add), "vco")
+    up(V.tensor_scalar(T.cst[:, 5:6], T.cst[:, 1:2], 16.5, None, OP.add), "vco")
+    up(V.tensor_scalar(T.cn[0:64, :], T.cc[0:64, :], -1.0, None, OP.mult), "vco")
+    wait("v", "vco")
+    up(V.tensor_scalar(T.wp[:], T.wm[:], T.cst[:, 3:4], -OUT, OP.mult, OP.add), "vco")
     wait("v", "ldw")
     up(V.quantize_mx(T.wq[:], T.wz[:], T.wt[:]), "wqd")
-    wait("v", "vcc")
-    wait("y", "qx", "oq")
-    up(Y.dma_start(u8("win0", 0, NQ), u8("qa0", 0, NQ)), "qc0", 16)
-    up(Y.dma_start(T.wis0[:, 0:NQ], T.qz0[:]), "qc0", 16)
-
-    def rows(out, view, sem_in, sem_out):
-        wait("g", sem_in)
-        for k in range(4):
-            up(g.partition_broadcast(out[:, 32 * k:32 * k + 32], view(32 * k, 32 * k + 1), 128), sem_out)
-
-    def wrap(row, f, x, y, out, vc, sem):
-        up(V.tensor_tensor(f(x), row, T.wm[:], OP.mult), vc)
-        wait("v", vc)
-        up(V.tensor_tensor_scan(f(y), T.nwm[:], f(x), 0.0, OP.mult, OP.add), vc)
-        wait("v", vc)
-        up(V.tensor_copy(out[:], f(y, 15, 128, 16)), sem)
+    wait("v", "vco")
+    wait("s", "vco")
 
     for t in range(R):
         def B(name, u=t):
@@ -202,12 +199,34 @@ def rank_program(g, core, T, topo):
             o, w = AT[name]
             return T["f%d" % u][:, o + a:o + (w if b is None else b):step]
 
-        def fr(name, u=t):
+        def h(name, a=0, b=None, step=1, p=0, n=32):
             o, w = AT[name]
-            return lambda p, q: T["f%d" % u][p:q, o:o + w]
+            return B("f")[p:p + n, o + a:o + (w if b is None else b):step]
+
+        def fold(row, block, sem):
+            for p in QUARTERS:
+                up(V.transpose(row[0:32, p:p + 32], h(block, p=p)), sem)
+
+        def lanes(out, y, sem):
+            for p in QUARTERS:
+                up(V.tensor_copy(out[p:p + 32, 0:8], h(y, 15, 128, 16)), sem)
+
+        def number(step, u=t):
+            where = T.land1[:, 1:32:4] if u == 0 else T.lidx[:, 0:32:4]
+            one, vw = (0, 1, 1, u), s("vw", u)
+            wait("v", vw)
+            if step == 0:
+                up(V.tensor_tensor(f("ol", 0, 8, 1, u), f("oh", 0, 8, 1, u), where, OP.mult), vw)
+            elif step == 1:
+                up(V.tensor_reduce(f("ix", *one), f("ol", 0, 8, 1, u), AX, OP.add), vw)
+            elif step == 2:
+                up(V.tensor_scalar(f("gg", *one), f("tw", *one), float(M), f("ix", *one), OP.mult, OP.add), vw)
+            else:
+                up(V.tensor_scalar(B("wv", u)[:, 0:1], f("gg", *one), f("b2", *one), f("b1", *one), OP.mult, OP.add),
+                   s("wi", u))
 
         one = (0, 1)
-        vc = s("vc")
+        va, vu, vb, vk, vc, vm = s("va"), s("vu"), s("vb"), s("vk"), s("vc"), s("vm")
         mq, mz, qa, qz = B("mq"), B("mz"), B("qa"), B("qz")
         if t == 0:
             wait("t", "mq0", "oq", "qx")
@@ -220,51 +239,52 @@ def rank_program(g, core, T, topo):
         for b in (0, 2, 1, 3):
             P.matmul_mx(T.pbl[:, 512 * b:512 * b + NQ], T.eq[:, 128 * b:128 * b + 128], T.ez[:, 128 * b:128 * b + 128],
                         qa[:], qz[:], True, False)
-        run = B("run")
+        run, land, k = B("run"), B("land"), 4 * rank
         wait("v", s("sc"))
         up(V.tensor_tensor_scan(run[:, 0:M], T.psc[:, 0:M], T.zz[:], LOW, OP.max, OP.add), s("rn"))
-        land = B("land")
-        k = 4 * rank
+        wait("g", s("rn"))
         if t == 0:
-            wait("g", s("rn"))
             send(run[:, M - 1:M], land[:, k:k + 1], s("ar"))
         else:
-            wait("g", s("ow", 0), s("rn"))
+            wait("g", "orn")
             send(run[:, M - 1:M + 1], land[:, k:k + 2], s("ar"))
         wait("s", s("rn"))
         up(S.activation(f("sg"), run[:, 0:M], AF.Sign, bias=run[:, M - 1:M], scale=-1.0, accum_out=f("ti", *one)), s("ix"))
         up(S.activation(land[:, k:k + 1], run[:, M - 1:M], AF.Copy), s("ow"))
-        wait("s", s("ix"))
         if t == 0:
-            up(S.activation(T.run1[:, M:M + 1], f("ti", *one), AF.Copy), s("ow"))
-            up(S.activation(T.land1[:, k + 1:k + 2], f("ti", *one), AF.Copy), s("ow"))
+            wait("v", "oq", "qx")
+            wait("s", "oq", "qx")
+            up(V.tensor_copy(u32("win0", 0, NQ), u32("qa0", 0, NQ).indirect(T.idl[:, 0:8])), s("qc"))
+            up(S.activation(T.wis0[:, 0:NQ], T.qz0[:, 0:NQ].indirect(T.idl[:, 0:8]), AF.Copy), s("qc"))
         else:
-            up(S.activation(T.lidx[:, k:k + 1], f("ti", *one), AF.Copy), "oli")
-        wait("v", s("ix"))
-        up(V.transpose(f("tit"), f("ti")), s("it"))
-        ri = B("ri")
-        rows(ri, fr("tit"), s("it"), s("ib"))
-        if t:
+            up(V.tensor_copy(u32("win1", 0, NQ), u32("win0", 0, NQ + N * E).indirect(T.offq0[:, 0:8])), s("qc"))
+            up(S.activation(T.wis1[:, 0:NQ], T.wis0[:, 0:NQ + N * E].indirect(T.offq0[:, 0:8]), AF.Copy), s("qc"))
             wait("g", s("ix"))
             send(f("ti", *one), T.lidx[:, k:k + 1], "idx")
-        wait("v", s("ib"))
-        wrap(ri[:, 0:128], f, "wx", "wy", B("offi"), vc, s("oi"))
+            wait("y", s("mp", 0), s("ar"))
+            up(Y.dma_start(u8("mw1", 0, M), u8("mq1", 0, M)), "mc1", 16)
+            up(Y.dma_start(T.mx1[:, 0:M], T.mz1[:]), "mc1", 16)
+        wait("v", s("ix"))
+        up(V.tensor_scalar(f("ra"), T.wm[:], f("ti", *one), None, OP.mult), va)
+        up(V.tensor_scalar(f("ru"), T.zz[:, 0:32], f("ti", *one), None, OP.add), vu)
+        wait("v", va)
+        fold(f("la"), "ra", va)
+        wait("v", va)
+        up(V.tensor_tensor_scan(h("ly"), T.nwm[0:32, :], h("la"), 0.0, OP.mult, OP.add), va)
+        wait("v", va)
+        lanes(B("offi"), "ly", s("oi"))
         wait("v", s("oi"))
         up(V.tensor_copy(u32(s("pm"), 0, NQ), u32(s("mq"), 0, M).indirect(B("offi")[:, 0:8])), s("pm"))
         wait("s", s("oi"))
         up(S.activation(B("pz")[:, 0:NQ], mz[:, 0:M].indirect(B("offi")[:, 0:8]), AF.Copy), s("pm"))
+        ri = B("ri")
+        wait("v", vu)
+        fold(ri, "ru", vu)
         wait("t", s("pm"))
         bank = {0: s("ba"), 1: s("bb"), 2: s("bc"), 3: s("bd")}
         for b in (0, 2, 1, 3):
             up(P.matmul_mx(T.pbl[:, 512 * b:512 * b + NQ], T.eq[:, 128 * b:128 * b + 128], T.ez[:, 128 * b:128 * b + 128],
                            B("pm")[:], B("pz")[:], False, True), bank[b])
-        wait("v", s("ow"), s("ar"))
-        up(V.tensor_tensor_scan(f("rl"), land[:, 0:32:4], T.zz[:, 0:8], LOW, OP.max, OP.add), s("rl"))
-        wait("s", s("rl"))
-        up(S.activation(f("sl"), f("rl"), AF.Sign, bias=f("rl", 7, 8), scale=-1.0, accum_out=f("tw", *one)), s("wr"))
-        wait("v", s("wr"))
-        up(V.transpose(f("twt"), f("tw")), s("wt"))
-        rows(f("rw"), fr("twt"), s("wt"), s("wb"))
         nt = B("nt")
         for b in (0, 1):
             wait("v", bank[b])
@@ -274,108 +294,131 @@ def rank_program(g, core, T, topo):
             up(S.activation(nt[:, b:512:4], T.pbl[:, 512 * b:512 * b + NQ], AF.Copy), s("nt"))
         wait("v", s("nt"))
         up(V.quantize_mx(B("nq")[:, 0:130], B("nz")[:, 0:130], nt[:]), s("nq"))
-        wait("v", s("wb"))
-        up(V.tensor_scalar(f("fl"), f("rw"), float(rank), None, OP.is_equal), vc)
+        wait("v", vu)
+        up(V.tensor_copy(ri[32:64, 0:NQ], ri[0:32, 0:NQ]), vu)
+        wait("s", s("ix"))
+        if t == 0:
+            up(S.activation(T.run1[:, M:M + 1], f("ti", *one), AF.Copy), "orn")
+            up(S.activation(T.land1[:, k + 1:k + 2], f("ti", *one), AF.Copy), "orn")
+        else:
+            up(S.activation(T.lidx[:, k:k + 1], f("ti", *one), AF.Copy), "oli")
+        wait("v", s("ow"), s("ar"))
+        up(V.tensor_tensor_scan(f("rl"), land[:, 0:32:4], T.zz[:, 0:8], LOW, OP.max, OP.add), vb)
+        wait("v", vb)
+        up(V.tensor_scalar(f("sl", 1, 9), f("rl"), f("rl", 7, 8), None, OP.is_lt), vb)
+        wait("v", vb)
+        up(V.tensor_scalar(f("fr"), T.zz[:, 0:32], f("sl", rank, rank + 1), f("sl", rank + 1, rank + 2), OP.add,
+                           OP.subtract), vb)
+        up(V.tensor_tensor(f("oh", 0, 8), f("sl", 0, 8), f("sl", 1, 9), OP.subtract), vc)
+        wait("v", vb)
+        fold(f("ft"), "fr", vb)
+        up(V.tensor_reduce(f("tw", *one), f("sl", 1, 9), AX, OP.add), vk)
+        wait("v", vb)
+        up(V.tensor_tensor_scan(h("cn"), h("ft"), T.zz[0:32, 0:128], 0.0, OP.add, OP.add), vb)
+        wait("s", vb)
+        up(S.activation(h("sa"), h("cn"), AF.Sign, bias=T.cst[0:32, 4:5], scale=-1.0, accum_out=h("acc", 0, 1)), s("ac"))
+        up(S.activation(h("sb"), h("cn"), AF.Sign, bias=T.cst[0:32, 5:6], scale=-1.0, accum_out=h("acc", 1, 2)), s("ac"))
         wait("v", vc)
-        up(V.tensor_tensor_scan(f("cn"), f("fl"), T.zz[:, 0:128], 0.0, OP.add, OP.add), s("ct"))
-        wait("s", s("ct"))
-        up(S.activation(f("sa"), f("cn"), AF.Sign, bias=T.cst[:, 4:5], scale=-1.0, accum_out=f("acc", 0, 1)), s("ac"))
-        up(S.activation(f("sb"), f("cn"), AF.Sign, bias=T.cst[:, 5:6], scale=-1.0, accum_out=f("acc", 1, 2)), s("ac"))
-        wait("v", s("nq"), s("mc"), s("ac"))
+        fold(f("ot"), "oh", vc)
+        wait("v", vc)
+        up(V.tensor_tensor_scan(h("ct"), h("ot"), T.zz[0:32, 0:128], 0.0, OP.add, OP.add), vc)
+        wait("v", s("ac"), s("nq"))
         offs = B("offs")
-        up(V.tensor_scalar(offs[:, 0:2], f("acc", 0, 2), 0.5, 64.0, OP.mult, OP.add), s("os"))
+        for p in QUARTERS:
+            up(V.tensor_scalar(offs[p:p + 32, 0:2], h("acc", 0, 2), 0.5, 64.0, OP.mult, OP.add), s("os"))
         wait("v", s("os"))
         up(V.tensor_copy(u32(s("mw"), M, M + E), u32(s("nq"), 0, 130).indirect(offs[:, 0:2])), s("sl"))
-        wait("s", s("nq"), s("mc"), s("os"))
+        wait("s", s("nq"), s("os"))
         up(S.activation(B("mx")[:, M:M + E], B("nz")[:, 0:130].indirect(offs[:, 0:2]), AF.Copy), s("sl"))
         wait("g", s("sl"))
         e = NQ + E * rank
         send(u8(s("mw"), M, M + E), u8(s("win"), e, e + E), s("nx"))
         send(B("mx")[:, M:M + E], B("wis")[:, e:e + E], s("nx"))
-        wait("y", s("sl"))
-        up(Y.dma_start(u8(s("win"), e, e + E), u8(s("mw"), M, M + E)), s("on"), 16)
-        up(Y.dma_start(B("wis")[:, e:e + E], B("mx")[:, M:M + E]), s("on"), 16)
-        w = f("tw", *one)
-        wait("v", "gtr")
-        up(V.tensor_scalar(f("eqm"), f("rw"), w, None, OP.is_equal), vc)
-        up(V.tensor_scalar(f("t1", *one), w, float(E), T.cst[:, 2:3], OP.mult, OP.add), vc)
+        wait("v", vu)
         up(V.tensor_tensor(B("uu")[:, 0:E], ri[:, 0:136].indirect(offs[:, 0:2]), T.kq[:], OP.add), s("u1"))
-        wait("v", vc)
-        up(V.tensor_tensor(f("eqt"), f("eqm"), T.tri[:], OP.mult), vc)
-        wait("v", vc)
-        up(V.tensor_reduce(f("kk", *one), f("eqt"), AX, OP.add), vc)
-        wait("v", vc)
-        up(V.tensor_scalar(f("an", *one), f("kk", *one), float(E), None, OP.is_lt), vc)
-        wait("v", vc)
-        up(V.tensor_scalar(f("tt", *one), f("kk", *one), f("t1", *one), f("an", *one), OP.add, OP.mult), vc)
-        wait("v", vc)
-        up(V.tensor_scalar(f("to", *one), f("tt", *one), T.cst[:, 0:1], None, OP.add), vc)
-        wait("v", vc)
-        up(V.transpose(f("tot"), f("to")), s("ot"))
-        rows(f("ro"), fr("tot"), s("ot"), s("ob"))
         wait("s", s("u1"))
-        for c in range(16):
-            up(S.activation(f("ab", 32 * c, 32 * c + 32), B("uu")[:, 0:E], AF.Abs, bias=T.cn[:, c:c + 1], scale=1.0), s("ab"))
+        for c in range(8):
+            up(S.activation(h("ab", 32 * c, 32 * c + 32, n=64), B("uu")[0:64, 0:E], AF.Abs, bias=T.cn[0:64, c:c + 1],
+                            scale=1.0), s("ab"))
+        up(S.activation(B("wis")[:, e:e + E], B("nz")[:, 0:130].indirect(offs[:, 0:2]), AF.Copy), s("on"))
+        wait("v", vc)
+        for p in QUARTERS:
+            up(V.transpose(h("cb", p=p), h("ct", p, p + 32)), vc)
+        wait("v", vk)
+        up(V.tensor_scalar(f("t1", *one), f("tw", *one), float(E), T.cst[:, 2:3], OP.mult, OP.add), vk)
+        wait("v", vc)
+        up(V.tensor_tensor(f("kr"), f("cb", 0, 8), f("oh", 0, 8), OP.mult), vc)
+        up(V.tensor_copy(u32(s("win"), e, e + E), u32(s("nq"), 0, 130).indirect(offs[:, 0:2])), s("on"))
+        wait("v", vc)
+        up(V.tensor_reduce(f("kk", *one), f("kr"), AX, OP.add), vc)
+        if t:
+            wait("v", "orn")
+            number(0, 0)
+        wait("v", vc)
+        up(V.tensor_scalar(f("an", *one), f("kk", *one), E + 0.5, None, OP.is_lt), vc)
+        if t:
+            number(1, 0)
+        wait("v", vc, vk)
+        up(V.tensor_scalar(f("tt", *one), f("kk", *one), f("t1", *one), f("an", *one), OP.add, OP.mult), vc)
+        up(V.tensor_scalar(f("b2", *one), f("an", *one), 2.0, -1.0, OP.mult, OP.add), s("vw"))
+        up(V.tensor_scalar(f("b1", *one), f("an", *one), -1.0, None, OP.add), s("vw"))
+        wait("v", vc)
+        up(V.tensor_scalar(f("rc"), T.wp[:], f("tt", *one), 0.0, OP.add, OP.max), vc)
+        if t:
+            number(2, 0)
+        wait("v", vc)
+        fold(f("lc"), "rc", vc)
+        if t:
+            number(3, 0)
         wait("v", s("ab"))
-        up(V.tensor_tensor_scan(f("am"), T.rst[:], f("ab"), 0.0, OP.max, OP.min), vc)
+        up(V.tensor_tensor_scan(h("am", n=64), T.rst[0:64, :], h("ab", n=64), 0.0, OP.max, OP.min), vm)
         wait("v", vc)
-        low = f("am", 31, 512, 32)
-        up(V.tensor_scalar(f("m1"), low, 0.5, None, OP.is_lt), vc)
-        up(V.tensor_scalar(f("m2"), low, 64.0, float(M), OP.mult, OP.add), vc)
+        up(V.tensor_tensor_scan(h("oy"), T.nwm[0:32, :], h("lc"), 0.0, OP.mult, OP.add), vc)
+        wait("v", vm)
+        low = h("am", 31, 256, 32, n=64)
+        up(V.tensor_scalar(h("m1", n=64), low, 0.5, None, OP.is_lt), vm)
+        up(V.tensor_scalar(h("m2", n=64), low, 64.0, float(M), OP.mult, OP.add), vm)
+        if t:
+            wait("v", "idx", "oli")
+            number(0, 1)
+        wait("v", vm)
+        up(V.tensor_tensor(h("m3", n=64), h("m1", n=64), h("m2", n=64), OP.mult), vm)
+        if t:
+            number(1, 1)
+        wait("v", vm)
+        up(V.tensor_tensor(h("m4", n=64), h("m3", n=64), T.cc[0:64, :], OP.max), vm)
         wait("v", vc)
-        up(V.tensor_tensor(f("m3"), f("m1"), f("m2"), OP.mult), vc)
-        wait("v", vc)
-        up(V.tensor_tensor(f("m4"), f("m3"), T.cp[:], OP.max), vc)
-        wait("v", vc)
-        up(V.tensor_copy(B("offm")[:], f("m4")), s("om"))
-        wait("v", s("ob"))
-        wrap(f("ro"), f, "ox", "oy", B("offq"), vc, s("od"))
-        wait("v", s("om"), s("sl"))
+        lanes(B("offq"), "oy", s("od"))
+        wait("v", vm)
+        for p in QUARTERS:
+            up(V.tensor_copy(B("offm")[p:p + 32, 0:8], h("m4")), s("om"))
+            up(V.tensor_copy(B("offm")[p:p + 32, 8:16], h("m4", p=32)), s("om"))
+        if t:
+            number(2, 1)
+            number(3, 1)
+        wait("v", s("om"), s("sl"), s("mc"))
         mp = s("mp")
         up(V.tensor_copy(u32(s("mq", t + 1), 0, M), u32(s("mw"), 0, M + E).indirect(B("offm")[:, 0:16])), mp)
-        wait("s", s("om"), s("sl"))
+        wait("s", s("om"), s("sl"), s("mc"))
         up(S.activation(B("mz", t + 1)[:, 0:M], B("mx")[:, 0:M + E].indirect(B("offm")[:, 0:16]), AF.Copy), mp)
-        wait("y", mp)
-        if t + 1 < R:
-            up(Y.dma_start(u8("mw1", 0, M), u8("mq1", 0, M)), "mc1", 16)
-            up(Y.dma_start(T.mx1[:, 0:M], T.mz1[:]), "mc1", 16)
-        else:
-            up(Y.dma_start(T.oc[:, 0:4 * M], u8(s("mq", R), 0, M)), "st", 16)
-            for c in range(4):
-                up(Y.dma_start(T.osc[4 * c:4 * c + 4, 0:M], B("mz", R)[32 * c:32 * c + 4, 0:M]), "st", 16)
-            wait("v", "idx", "oli")
-            for u in range(R):
-                where = T.land1[:, 1:32:4] if u == 0 else T.lidx[:, 0:32:4]
-                wu, au = f("tw", 0, 1, 1, u), f("an", 0, 1, 1, u)
-                up(V.tensor_scalar(f("oh", 0, 8, 1, u), T.kf[:, 0:8], wu, None, OP.is_equal), vc)
-                up(V.tensor_scalar(f("b2", 0, 1, 1, u), au, 2.0, -1.0, OP.mult, OP.add), vc)
-                up(V.tensor_scalar(f("b1", 0, 1, 1, u), au, -1.0, None, OP.add), vc)
-                wait("v", vc)
-                up(V.tensor_tensor(f("ol", 0, 8, 1, u), f("oh", 0, 8, 1, u), where, OP.mult), vc)
-                wait("v", vc)
-                up(V.tensor_reduce(f("ix", 0, 1, 1, u), f("ol", 0, 8, 1, u), AX, OP.add), vc)
-                wait("v", vc)
-                up(V.tensor_scalar(f("gg", 0, 1, 1, u), wu, float(M), f("ix", 0, 1, 1, u), OP.mult, OP.add), vc)
-                wait("v", vc)
-                up(V.tensor_scalar(B("wv", u)[:, 0:1], f("gg", 0, 1, 1, u), f("b2", 0, 1, 1, u), f("b1", 0, 1, 1, u),
-                                   OP.mult, OP.add), s("wi", u))
-                wait("y", s("wi", u))
-                up(Y.dma_start(T.wi[u:u + 1, :], B("wv", u)[:, 0:1]), "st", 16)
         for q in ("v", "s"):
             wait(q, s("od"), s("on"), s("qc"), s("nx"))
         up(V.tensor_copy(u32(s("qa", t + 1), 0, NQ), u32(s("win"), 0, NQ + N * E).indirect(B("offq")[:, 0:8])), s("qp"))
         up(S.activation(B("qz", t + 1)[:, 0:NQ], B("wis")[:, 0:NQ + N * E].indirect(B("offq")[:, 0:8]), AF.Copy), s("qp"))
-        if t + 1 < R:
-            wait("y", s("qp"))
-            up(Y.dma_start(u8("win1", 0, NQ), u8("qa1", 0, NQ)), "qc1", 16)
-            up(Y.dma_start(T.wis1[:, 0:NQ], T.qz1[:]), "qc1", 16)
 
+    wait("y", "wi0", "wi1")
+    for u in range(R):
+        up(Y.dma_start(T.wi[u:u + 1, :], T["wv%d" % u][:, 0:1]), "st", 16)
+    wait("y", "mp1", "nx1")
+    up(Y.dma_start(T.oc[:, 0:4 * M], u8("mq%d" % R, 0, M)), "st", 16)
+    for c in range(4):
+        up(Y.dma_start(T.osc[4 * c:4 * c + 4, 0:M], T["mz%d" % R][32 * c:32 * c + 4, 0:M]), "st", 16)
     wait("t", "wqd", "qp1")
     up(P.matmul_mx(T.pyy[:, 0:NQ], T.wq[:], T.wz[:], T.qa2[:], T.qz2[:], True, True), "yp")
     wait("v", "yp")
     up(V.tensor_copy(T.yt[:], T.pyy[:, 0:NQ]), "yc")
-    wait("y", "yc")
-    up(Y.dma_start(T.y[:], T.yt[:]), "st", 16)
+    wait("s", "yc")
+    up(S.dma_start(T.y[:], T.yt[:]), "sty", 16)
     for name in total:
         if seen.get(("", name), 0) < total[name]:
             wait("g", name)

from concourse.bass import DstId, RemoteDMATransfer
from concourse.mybir import dt, AluOpType, AxisListType, ActivationFunctionType

N, M, A, E, R = 8, 256, 16, 32, 2
NQ = N * A
OP = AluOpType
AF = ActivationFunctionType
AX = AxisListType.X
BIG = 1.0e9
LOW = -9.0e29
OUT = 65536.0

WORK = [("ti", 8), ("sl", 16), ("ra", 32), ("ru", 32), ("fr", 32), ("oh", 32), ("cb", 32), ("rc", 32), ("la", 128),
        ("ly", 128), ("ft", 128), ("cn", 128), ("sa", 128), ("sb", 128), ("acc", 8), ("ot", 128), ("ct", 128), ("lc", 128),
        ("oy", 128), ("rl", 8), ("tw", 8), ("t1", 8), ("kr", 8), ("kk", 8), ("an", 8), ("tt", 8), ("m1", 8), ("m2", 8),
        ("m3", 8), ("m4", 8), ("ol", 8), ("ix", 8), ("gg", 8), ("b1", 8), ("b2", 8), ("sg", 256), ("ab", 256), ("am", 256)]
AT = {}
_n = 0
for _name, _w in WORK:
    AT[_name] = (_n, _w)
    _n += _w

SCRATCH = {
    "xt": ("sbuf", [128, 512], "bfloat16"), "met": ("sbuf", [128, 4 * M], "bfloat16"),
    "wt": ("sbuf", [128, 512], "bfloat16"), "et": ("sbuf", [128, 2048], "bfloat16"),
    "half": ("sbuf", [128, 128], "bfloat16"), "diag": ("sbuf", [128, 128], "bfloat16"),
    "xq": ("sbuf", [128, 128], "float8_e4m3fn_x4"), "xs": ("sbuf", [128, 128], "uint8"),
    "wq": ("sbuf", [128, 128], "float8_e4m3fn_x4"), "wz": ("sbuf", [128, 128], "uint8"),
    "eq": ("sbuf", [128, 512], "float8_e4m3fn_x4"), "ez": ("sbuf", [128, 512], "uint8"),
    "zz": ("sbuf", [128, 256], "float32"), "wm": ("sbuf", [128, 32], "float32"), "nwm": ("sbuf", [128, 128], "float32"),
    "wp": ("sbuf", [128, 32], "float32"),
    "rst": ("sbuf", [128, 256], "float32"), "lp": ("sbuf", [128, 128], "int32"), "la": ("sbuf", [128, 128], "int32"),
    "ip": ("sbuf", [128, 8], "int32"), "ia": ("sbuf", [128, 8], "int32"), "kf": ("sbuf", [128, 32], "float32"),
    "kq": ("sbuf", [128, 32], "float32"), "c16": ("sbuf", [128, 16], "float32"), "cp": ("sbuf", [128, 16], "float32"),
    "cc": ("sbuf", [128, 8], "float32"), "cn": ("sbuf", [128, 8], "float32"),
    "cst": ("sbuf", [128, 32], "float32"), "yt": ("sbuf", [128, 128], "float32"),
    "idl": ("sbuf", [128, 16], "uint16"), "lidx": ("sbuf", [128, 32], "float32"),
    "psc": ("psum", [128, 512], "float32"), "pbl": ("psum", [128, 2048], "float32"), "pyy": ("psum", [128, 512], "float32"),
}
for _t in range(R + 1):
    SCRATCH["mq%d" % _t] = ("sbuf", [128, M], "float8_e4m3fn_x4")
    SCRATCH["mz%d" % _t] = ("sbuf", [128, M], "uint8")
    SCRATCH["qa%d" % _t] = ("sbuf", [128, NQ], "float8_e4m3fn_x4")
    SCRATCH["qz%d" % _t] = ("sbuf", [128, NQ], "uint8")
for _t in range(R):
    for _name, _w, _d in (("mw", M + E, "float8_e4m3fn_x4"), ("mx", M + E, "uint8"),
                          ("win", NQ + N * E, "float8_e4m3fn_x4"), ("wis", NQ + N * E, "uint8"),
                          ("pm", NQ, "float8_e4m3fn_x4"), ("pz", NQ, "uint8"),
                          ("nq", 160, "float8_e4m3fn_x4"), ("nz", 160, "uint8"),
                          ("nt", 520, "bfloat16"), ("run", 264, "float32"), ("land", 32, "float32"),
                          ("ri", 136, "float32"), ("uu", 32, "float32"), ("wv", 8, "float32"), ("f", _n, "float32"),
                          ("offi", 8, "uint16"), ("offs", 2, "uint16"), ("offm", 16, "uint16"), ("offq", 8, "uint16")):
        SCRATCH["%s%d" % (_name, _t)] = ("sbuf", [128, _w], _d)

ONCE = ["ldx", "ldm", "ldw", "ixt", "ihf", "gdi", "gip", "xqd", "eqd", "wqd", "qx", "oq", "mq0", "vcc", "vco", "vid",
        "ls", "idx", "oli", "orn", "yp", "yc", "st", "sty"]
EACH = ["sc", "rn", "ix", "ow", "oi", "pm", "ba", "bb", "bc", "bd", "nt", "nq", "ar", "ac", "os", "sl", "u1", "ab",
        "om", "mp", "od", "nx", "on", "qp", "mc", "qc", "wi", "va", "vu", "vb", "vk", "vc", "vm", "vw"]
SEMAPHORES = ONCE + ["%s%d" % (_s, _t) for _s in EACH for _t in range(R)]
QUARTERS = (0, 32, 64, 96)


def rank_program(g, core, T, topo):
    rank = T.rank_of(core)
    if rank is None:
        return
    V, S, P, Y = g.vector, g.scalar, g.tensor, g.sync
    queue = {"v": V, "s": S, "t": P, "y": Y, "g": g}
    total, seen = {}, {}

    def up(ins, name, n=1):
        ins.then_inc(T.sem[name], n)
        total[name] = total.get(name, 0) + n

    def wait(q, *names):
        for name in names:
            if seen.get((q, name), 0) < total[name]:
                queue[q].wait_ge(T.sem[name], total[name])
                seen[(q, name)] = total[name]
                seen[("", name)] = total[name]

    def u32(name, a, b):
        return T[name][:, a:b].bitcast(dt.uint32)

    def u8(name, a, b):
        return T[name][:, a:b].bitcast(dt.uint8)

    here = topo.chip(core)

    def near(c):
        k = topo.chip(c)
        return (2 if topo.mates(here, k) else 1 if topo.same_plane(here, k) else 0, topo.die(c) != topo.die(core))

    off = sorted([c for c in T.cores if topo.chip(c) != here], key=near)
    on = [c for c in T.cores if c != core and topo.chip(c) == here]
    common = topo.mask(core, off[0])
    for c in off:
        common = common & topo.mask(core, c)
    free = [e for e in topo.engines(core, on[0]) if not common >> e & 1]
    local = (1 << free[0]) | (1 << free[len(free) // 2])
    n_off = sum(common >> e & 1 for e in range(common.bit_length()))
    arrive = len(off) * n_off + len(on) * 2

    def dst(c):
        rid, pid = topo.addr(c)[:2]
        return DstId(rid=rid, pnc=pid)

    def send(src, out, sem):
        g.remote_dma_fused([
            RemoteDMATransfer(dst_ids=[dst(c) for c in off], dma_engine_mask=common, remote_sem=T.sem[sem],
                              srcs=[src], dsts=[out for c in off]),
            RemoteDMATransfer(dst_ids=[dst(c) for c in on], dma_engine_mask=local, remote_sem=T.sem[sem],
                              srcs=[src], dsts=[out for c in on])], local_sem=T.sem["ls"])
        total["ls"] = total.get("ls", 0) + n_off + 2
        total[sem] = total.get(sem, 0) + arrive

    up(Y.dma_start(T.xt[:, 0:4 * A], T.x[:]), "ldx", 16)
    up(Y.dma_start(T.met[:], T.me[:]), "ldm", 16)
    up(Y.dma_start(T.wt[:], T.w[:]), "ldw", 16)

    up(V.memset(T.xt[:, 4 * A:512], 0.0), "ixt")
    up(V.memset(T.half[:], 0.5), "ihf")
    up(V.memset(T.et[:], 0.0), "vcc")
    up(g.iota(T.ip[:, 0:1], [[1, 1]], 0, 1), "gip")
    up(g.iota(T.c16[:], [[16, 16]], 0, 0, allow_small_or_imprecise_dtypes=True), "gip")
    up(g.iota(T.lp[:], [[1, 128]], 128, -1), "gip")
    up(g.iota(T.kf[:], [[1, 32]], 0, 0, allow_small_or_imprecise_dtypes=True), "gip")
    wait("g", "ihf")
    up(g.affine_select(T.diag[:], T.half[:], [[-1, 128]], OP.is_equal, 0.0, 0, 1), "gdi")
    wait("v", "ldx", "ixt")
    up(V.quantize_mx(T.xq[:], T.xs[:], T.xt[:]), "xqd")
    a = A * rank
    wait("g", "xqd")
    send(u8("xq", 0, A), u8("qa0", a, a + A), "qx")
    send(T.xs[:, 0:A], T.qz0[:, a:a + A], "qx")
    wait("g", "gip", "gdi")

    wait("v", "gip")
    up(V.tensor_scalar(T.ia[:, 0:1], T.ip[:, 0:1], 15, None, OP.bitwise_and), "vid")
    up(V.tensor_copy(T.cst[:, 0:1], T.ip[:, 0:1]), "vco")
    up(V.tensor_scalar(T.la[:], T.lp[:], 15, None, OP.bitwise_and), "vco")
    wait("v", "vid")
    up(V.tensor_copy(T.cst[:, 1:2], T.ia[:, 0:1]), "vid")
    wait("v", "vid")
    up(V.tensor_scalar(T.cp[:], T.c16[:], T.cst[:, 1:2], None, OP.add), "vid")
    wait("v", "vid")
    up(V.tensor_copy(T.idl[:], T.cp[:]), "vid")
    wait("v", "vid", "xqd")
    up(V.tensor_copy(u32("qa0", a, a + A), u32("xq", 0, NQ).indirect(T.idl[:, 0:1])), "oq")
    wait("s", "vid", "xqd")
    up(S.activation(T.qz0[:, a:a + A], T.xs[:, 0:NQ].indirect(T.idl[:, 0:1]), AF.Copy), "oq")
    wait("v", "vcc", "gdi")
    for b in range(4):
        up(V.tensor_copy(T.et[:, 512 * b + b:512 * b + 512:4], T.diag[:]), "vcc")
    up(V.memset(T.zz[:], 0.0), "vco")
    wait("v", "vcc")
    up(V.quantize_mx(T.eq[:], T.ez[:], T.et[:]), "eqd")
    wait("v", "ldm")
    up(V.quantize_mx(T.mq0[:], T.mz0[:], T.met[:]), "mq0")
    up(V.memset(T.rst[:], -BIG), "vco")
    for t in range(R):
        o = AT["oh"][0]
        up(V.memset(T["f%d" % t][:, o:o + 32], 0.0), "vco")
        o = AT["sl"][0]
        up(V.memset(T["f%d" % t][:, o:o + 1], 1.0), "vco")
        up(V.memset(T["ri%d" % t][:], 1000.0), "vco")
        up(V.memset(T["nt%d" % t][:, 512:520], 0.0), "vco")
    up(V.tensor_scalar(T.kq[:], T.kf[:], 1.0 / 64, None, OP.mult), "vco")
    up(V.tensor_copy(T.cc[0:32, :], T.cp[0:32, 0:8]), "vco")
    up(V.tensor_copy(T.cc[32:64, :], T.cp[32:64, 8:16]), "vco")
    wait("v", "mq0")
    up(V.tensor_copy(u32("mw0", 0, M), u32("mq0", 0, M).indirect(T.idl[:])), "mc0")
    wait("s", "mq0")
    up(S.activation(T.mx0[:, 0:M], T.mz0[:].indirect(T.idl[:]), AF.Copy), "mc0")
    wait("v", "vco")
    up(V.memset(T.rst[:, 0:256:32], BIG), "vco")
    up(V.tensor_scalar(T.wm[:], T.la[:, 0:32], 0, None, OP.is_equal), "vco")
    up(V.tensor_scalar(T.nwm[:], T.la[:], 0, None, OP.not_equal), "vco")
    up(V.tensor_scalar(T.cst[:, 2:3], T.cst[:, 0:1], -1.0, float(NQ - 1), OP.mult, OP.add), "vco")
    up(V.tensor_scalar(T.cst[:, 3:4], T.cst[:, 0:1], OUT, None, OP.add), "vco")
    up(V.tensor_scalar(T.cst[:, 4:5], T.cst[:, 1:2], 0.5, None, OP.add), "vco")
    up(V.tensor_scalar(T.cst[:, 5:6], T.cst[:, 1:2], 16.5, None, OP.add), "vco")
    up(V.tensor_scalar(T.cn[0:64, :], T.cc[0:64, :], -1.0, None, OP.mult), "vco")
    wait("v", "vco")
    up(V.tensor_scalar(T.wp[:], T.wm[:], T.cst[:, 3:4], -OUT, OP.mult, OP.add), "vco")
    wait("v", "ldw")
    up(V.quantize_mx(T.wq[:], T.wz[:], T.wt[:]), "wqd")
    wait("v", "vco")
    wait("s", "vco")

    for t in range(R):
        def B(name, u=t):
            return T["%s%d" % (name, u)]

        def s(name, u=t):
            return "%s%d" % (name, u)

        def f(name, a=0, b=None, step=1, u=t):
            o, w = AT[name]
            return T["f%d" % u][:, o + a:o + (w if b is None else b):step]

        def h(name, a=0, b=None, step=1, p=0, n=32):
            o, w = AT[name]
            return B("f")[p:p + n, o + a:o + (w if b is None else b):step]

        def fold(row, block, sem):
            for p in QUARTERS:
                up(V.transpose(row[0:32, p:p + 32], h(block, p=p)), sem)

        def lanes(out, y, sem):
            for p in QUARTERS:
                up(V.tensor_copy(out[p:p + 32, 0:8], h(y, 15, 128, 16)), sem)

        def number(step, u=t):
            where = T.land1[:, 1:32:4] if u == 0 else T.lidx[:, 0:32:4]
            one, vw = (0, 1, 1, u), s("vw", u)
            wait("v", vw)
            if step == 0:
                up(V.tensor_tensor(f("ol", 0, 8, 1, u), f("oh", 0, 8, 1, u), where, OP.mult), vw)
            elif step == 1:
                up(V.tensor_reduce(f("ix", *one), f("ol", 0, 8, 1, u), AX, OP.add), vw)
            elif step == 2:
                up(V.tensor_scalar(f("gg", *one), f("tw", *one), float(M), f("ix", *one), OP.mult, OP.add), vw)
            else:
                up(V.tensor_scalar(B("wv", u)[:, 0:1], f("gg", *one), f("b2", *one), f("b1", *one), OP.mult, OP.add),
                   s("wi", u))

        one = (0, 1)
        va, vu, vb, vk, vc, vm = s("va"), s("vu"), s("vb"), s("vk"), s("vc"), s("vm")
        mq, mz, qa, qz = B("mq"), B("mz"), B("qa"), B("qz")
        if t == 0:
            wait("t", "mq0", "oq", "qx")
        else:
            wait("t", s("mp", 0), s("rn", 0), s("qp", 0))
        up(P.matmul_mx(T.psc[:, 0:M], qa[:], qz[:], mq[:], mz[:], True, True), s("sc"))
        wait("t", "eqd")
        if t:
            wait("t", s("nt", 0))
        for b in (0, 2, 1, 3):
            P.matmul_mx(T.pbl[:, 512 * b:512 * b + NQ], T.eq[:, 128 * b:128 * b + 128], T.ez[:, 128 * b:128 * b + 128],
                        qa[:], qz[:], True, False)
        run, land, k = B("run"), B("land"), 4 * rank
        wait("v", s("sc"))
        up(V.tensor_tensor_scan(run[:, 0:M], T.psc[:, 0:M], T.zz[:], LOW, OP.max, OP.add), s("rn"))
        wait("g", s("rn"))
        if t == 0:
            send(run[:, M - 1:M], land[:, k:k + 1], s("ar"))
        else:
            wait("g", "orn")
            send(run[:, M - 1:M + 1], land[:, k:k + 2], s("ar"))
        wait("s", s("rn"))
        up(S.activation(f("sg"), run[:, 0:M], AF.Sign, bias=run[:, M - 1:M], scale=-1.0, accum_out=f("ti", *one)), s("ix"))
        up(S.activation(land[:, k:k + 1], run[:, M - 1:M], AF.Copy), s("ow"))
        if t == 0:
            wait("v", "oq", "qx")
            wait("s", "oq", "qx")
            up(V.tensor_copy(u32("win0", 0, NQ), u32("qa0", 0, NQ).indirect(T.idl[:, 0:8])), s("qc"))
            up(S.activation(T.wis0[:, 0:NQ], T.qz0[:, 0:NQ].indirect(T.idl[:, 0:8]), AF.Copy), s("qc"))
        else:
            up(V.tensor_copy(u32("win1", 0, NQ), u32("win0", 0, NQ + N * E).indirect(T.offq0[:, 0:8])), s("qc"))
            up(S.activation(T.wis1[:, 0:NQ], T.wis0[:, 0:NQ + N * E].indirect(T.offq0[:, 0:8]), AF.Copy), s("qc"))
            wait("g", s("ix"))
            send(f("ti", *one), T.lidx[:, k:k + 1], "idx")
            wait("y", s("mp", 0), s("ar"))
            up(Y.dma_start(u8("mw1", 0, M), u8("mq1", 0, M)), "mc1", 16)
            up(Y.dma_start(T.mx1[:, 0:M], T.mz1[:]), "mc1", 16)
        wait("v", s("ix"))
        up(V.tensor_scalar(f("ra"), T.wm[:], f("ti", *one), None, OP.mult), va)
        up(V.tensor_scalar(f("ru"), T.zz[:, 0:32], f("ti", *one), None, OP.add), vu)
        wait("v", va)
        fold(f("la"), "ra", va)
        wait("v", va)
        up(V.tensor_tensor_scan(h("ly"), T.nwm[0:32, :], h("la"), 0.0, OP.mult, OP.add), va)
        wait("v", va)
        lanes(B("offi"), "ly", s("oi"))
        wait("v", s("oi"))
        up(V.tensor_copy(u32(s("pm"), 0, NQ), u32(s("mq"), 0, M).indirect(B("offi")[:, 0:8])), s("pm"))
        wait("s", s("oi"))
        up(S.activation(B("pz")[:, 0:NQ], mz[:, 0:M].indirect(B("offi")[:, 0:8]), AF.Copy), s("pm"))
        ri = B("ri")
        wait("v", vu)
        fold(ri, "ru", vu)
        wait("t", s("pm"))
        bank = {0: s("ba"), 1: s("bb"), 2: s("bc"), 3: s("bd")}
        for b in (0, 2, 1, 3):
            up(P.matmul_mx(T.pbl[:, 512 * b:512 * b + NQ], T.eq[:, 128 * b:128 * b + 128], T.ez[:, 128 * b:128 * b + 128],
                           B("pm")[:], B("pz")[:], False, True), bank[b])
        nt = B("nt")
        for b in (0, 1):
            wait("v", bank[b])
            up(V.tensor_copy(nt[:, b:512:4], T.pbl[:, 512 * b:512 * b + NQ]), s("nt"))
        for b in (2, 3):
            wait("s", bank[b])
            up(S.activation(nt[:, b:512:4], T.pbl[:, 512 * b:512 * b + NQ], AF.Copy), s("nt"))
        wait("v", s("nt"))
        up(V.quantize_mx(B("nq")[:, 0:130], B("nz")[:, 0:130], nt[:]), s("nq"))
        wait("v", vu)
        up(V.tensor_copy(ri[32:64, 0:NQ], ri[0:32, 0:NQ]), vu)
        wait("s", s("ix"))
        if t == 0:
            up(S.activation(T.run1[:, M:M + 1], f("ti", *one), AF.Copy), "orn")
            up(S.activation(T.land1[:, k + 1:k + 2], f("ti", *one), AF.Copy), "orn")
        else:
            up(S.activation(T.lidx[:, k:k + 1], f("ti", *one), AF.Copy), "oli")
        wait("v", s("ow"), s("ar"))
        up(V.tensor_tensor_scan(f("rl"), land[:, 0:32:4], T.zz[:, 0:8], LOW, OP.max, OP.add), vb)
        wait("v", vb)
        up(V.tensor_scalar(f("sl", 1, 9), f("rl"), f("rl", 7, 8), None, OP.is_lt), vb)
        wait("v", vb)
        up(V.tensor_scalar(f("fr"), T.zz[:, 0:32], f("sl", rank, rank + 1), f("sl", rank + 1, rank + 2), OP.add,
                           OP.subtract), vb)
        up(V.tensor_tensor(f("oh", 0, 8), f("sl", 0, 8), f("sl", 1, 9), OP.subtract), vc)
        wait("v", vb)
        fold(f("ft"), "fr", vb)
        up(V.tensor_reduce(f("tw", *one), f("sl", 1, 9), AX, OP.add), vk)
        wait("v", vb)
        up(V.tensor_tensor_scan(h("cn"), h("ft"), T.zz[0:32, 0:128], 0.0, OP.add, OP.add), vb)
        wait("s", vb)
        up(S.activation(h("sa"), h("cn"), AF.Sign, bias=T.cst[0:32, 4:5], scale=-1.0, accum_out=h("acc", 0, 1)), s("ac"))
        up(S.activation(h("sb"), h("cn"), AF.Sign, bias=T.cst[0:32, 5:6], scale=-1.0, accum_out=h("acc", 1, 2)), s("ac"))
        wait("v", vc)
        fold(f("ot"), "oh", vc)
        wait("v", vc)
        up(V.tensor_tensor_scan(h("ct"), h("ot"), T.zz[0:32, 0:128], 0.0, OP.add, OP.add), vc)
        wait("v", s("ac"), s("nq"))
        offs = B("offs")
        for p in QUARTERS:
            up(V.tensor_scalar(offs[p:p + 32, 0:2], h("acc", 0, 2), 0.5, 64.0, OP.mult, OP.add), s("os"))
        wait("v", s("os"))
        up(V.tensor_copy(u32(s("mw"), M, M + E), u32(s("nq"), 0, 130).indirect(offs[:, 0:2])), s("sl"))
        wait("s", s("nq"), s("os"))
        up(S.activation(B("mx")[:, M:M + E], B("nz")[:, 0:130].indirect(offs[:, 0:2]), AF.Copy), s("sl"))
        wait("g", s("sl"))
        e = NQ + E * rank
        send(u8(s("mw"), M, M + E), u8(s("win"), e, e + E), s("nx"))
        send(B("mx")[:, M:M + E], B("wis")[:, e:e + E], s("nx"))
        wait("v", vu)
        up(V.tensor_tensor(B("uu")[:, 0:E], ri[:, 0:136].indirect(offs[:, 0:2]), T.kq[:], OP.add), s("u1"))
        wait("s", s("u1"))
        for c in range(8):
            up(S.activation(h("ab", 32 * c, 32 * c + 32, n=64), B("uu")[0:64, 0:E], AF.Abs, bias=T.cn[0:64, c:c + 1],
                            scale=1.0), s("ab"))
        up(S.activation(B("wis")[:, e:e + E], B("nz")[:, 0:130].indirect(offs[:, 0:2]), AF.Copy), s("on"))
        wait("v", vc)
        for p in QUARTERS:
            up(V.transpose(h("cb", p=p), h("ct", p, p + 32)), vc)
        wait("v", vk)
        up(V.tensor_scalar(f("t1", *one), f("tw", *one), float(E), T.cst[:, 2:3], OP.mult, OP.add), vk)
        wait("v", vc)
        up(V.tensor_tensor(f("kr"), f("cb", 0, 8), f("oh", 0, 8), OP.mult), vc)
        up(V.tensor_copy(u32(s("win"), e, e + E), u32(s("nq"), 0, 130).indirect(offs[:, 0:2])), s("on"))
        wait("v", vc)
        up(V.tensor_reduce(f("kk", *one), f("kr"), AX, OP.add), vc)
        if t:
            wait("v", "orn")
            number(0, 0)
        wait("v", vc)
        up(V.tensor_scalar(f("an", *one), f("kk", *one), E + 0.5, None, OP.is_lt), vc)
        if t:
            number(1, 0)
        wait("v", vc, vk)
        up(V.tensor_scalar(f("tt", *one), f("kk", *one), f("t1", *one), f("an", *one), OP.add, OP.mult), vc)
        up(V.tensor_scalar(f("b2", *one), f("an", *one), 2.0, -1.0, OP.mult, OP.add), s("vw"))
        up(V.tensor_scalar(f("b1", *one), f("an", *one), -1.0, None, OP.add), s("vw"))
        wait("v", vc)
        up(V.tensor_scalar(f("rc"), T.wp[:], f("tt", *one), 0.0, OP.add, OP.max), vc)
        if t:
            number(2, 0)
        wait("v", vc)
        fold(f("lc"), "rc", vc)
        if t:
            number(3, 0)
        wait("v", s("ab"))
        up(V.tensor_tensor_scan(h("am", n=64), T.rst[0:64, :], h("ab", n=64), 0.0, OP.max, OP.min), vm)
        wait("v", vc)
        up(V.tensor_tensor_scan(h("oy"), T.nwm[0:32, :], h("lc"), 0.0, OP.mult, OP.add), vc)
        wait("v", vm)
        low = h("am", 31, 256, 32, n=64)
        up(V.tensor_scalar(h("m1", n=64), low, 0.5, None, OP.is_lt), vm)
        up(V.tensor_scalar(h("m2", n=64), low, 64.0, float(M), OP.mult, OP.add), vm)
        if t:
            wait("v", "idx", "oli")
            number(0, 1)
        wait("v", vm)
        up(V.tensor_tensor(h("m3", n=64), h("m1", n=64), h("m2", n=64), OP.mult), vm)
        if t:
            number(1, 1)
        wait("v", vm)
        up(V.tensor_tensor(h("m4", n=64), h("m3", n=64), T.cc[0:64, :], OP.max), vm)
        wait("v", vc)
        lanes(B("offq"), "oy", s("od"))
        wait("v", vm)
        for p in QUARTERS:
            up(V.tensor_copy(B("offm")[p:p + 32, 0:8], h("m4")), s("om"))
            up(V.tensor_copy(B("offm")[p:p + 32, 8:16], h("m4", p=32)), s("om"))
        if t:
            number(2, 1)
            number(3, 1)
        wait("v", s("om"), s("sl"), s("mc"))
        mp = s("mp")
        up(V.tensor_copy(u32(s("mq", t + 1), 0, M), u32(s("mw"), 0, M + E).indirect(B("offm")[:, 0:16])), mp)
        wait("s", s("om"), s("sl"), s("mc"))
        up(S.activation(B("mz", t + 1)[:, 0:M], B("mx")[:, 0:M + E].indirect(B("offm")[:, 0:16]), AF.Copy), mp)
        for q in ("v", "s"):
            wait(q, s("od"), s("on"), s("qc"), s("nx"))
        up(V.tensor_copy(u32(s("qa", t + 1), 0, NQ), u32(s("win"), 0, NQ + N * E).indirect(B("offq")[:, 0:8])), s("qp"))
        up(S.activation(B("qz", t + 1)[:, 0:NQ], B("wis")[:, 0:NQ + N * E].indirect(B("offq")[:, 0:8]), AF.Copy), s("qp"))

    wait("y", "wi0", "wi1")
    for u in range(R):
        up(Y.dma_start(T.wi[u:u + 1, :], T["wv%d" % u][:, 0:1]), "st", 16)
    wait("y", "mp1", "nx1")
    up(Y.dma_start(T.oc[:, 0:4 * M], u8("mq%d" % R, 0, M)), "st", 16)
    for c in range(4):
        up(Y.dma_start(T.osc[4 * c:4 * c + 4, 0:M], T["mz%d" % R][32 * c:32 * c + 4, 0:M]), "st", 16)
    wait("t", "wqd", "qp1")
    up(P.matmul_mx(T.pyy[:, 0:NQ], T.wq[:], T.wz[:], T.qa2[:], T.qz2[:], True, True), "yp")
    wait("v", "yp")
    up(V.tensor_copy(T.yt[:], T.pyy[:, 0:NQ]), "yc")
    wait("s", "yc")
    up(S.dma_start(T.y[:], T.yt[:]), "sty", 16)
    for name in total:
        if seen.get(("", name), 0) < total[name]:
            wait("g", name)
